import numpy as np
import ml_dtypes


def mxq(x, axis, fmt="e4m3"):
    dtype, down = {"e4m3": (ml_dtypes.float8_e4m3fn, 7), "e5m2": (ml_dtypes.float8_e5m2, 14)}[fmt]
    v = np.moveaxis(np.asarray(x, np.float32).astype(ml_dtypes.bfloat16).astype(np.float64), axis, -1)
    blocks = v.reshape(v.shape[:-1] + (-1, 32))
    amax = np.abs(blocks).max(-1, keepdims=True)
    byte = np.maximum(np.where(amax > 0, np.frexp(amax)[1] - 1 + 127, 0) - down, 1)
    scale = np.exp2(byte - 127.0)
    codes = (blocks / scale).astype(np.float32).astype(dtype).astype(np.float64)
    return np.moveaxis((codes * scale).reshape(v.shape), -1, axis)


WIDE = False


def mx_kscale(k):
    if not WIDE:
        return np.ones(k)
    levels = np.array([10, -10, 5, -5, 0])
    if k % 512:
        return np.exp2(np.random.permutation(np.resize(levels, k // 32))).repeat(32)
    a = np.empty((k // 512, 16))
    for p in range(k // 512):
        a[p, :8] = np.random.permutation(np.resize(levels, 8))
        for g in range(8):
            far = levels[np.abs(levels - a[p, g]) >= 10]
            a[p, g + 8] = far[np.random.randint(len(far))]
    return np.exp2(a.ravel()).repeat(32)


def f64(x):
    return np.asarray(x).astype(np.float64)


E2M1 = np.array([0.0, 0.5, 1.0, 1.5, 2.0, 3.0, 4.0, 6.0, -0.0, -0.5, -1.0, -1.5, -2.0, -3.0, -4.0, -6.0])


def pack_weight(w, fmt):
    k, n = w.shape
    w = f64(np.asarray(w, np.float32).astype(ml_dtypes.bfloat16)).reshape(k // 32, 32, n)
    amax = np.abs(w).max(1)
    if fmt == "e4m3":
        byte = np.frexp(amax)[1] - 1 + 127 - 7
    else:
        mant, ex = np.frexp(amax / 6.0)
        byte = np.where(mant > 0.5, ex, ex - 1) + 127
    byte = np.clip(np.where(amax > 0, byte, 1), 1, 254)
    scaled = (w * np.exp2(127.0 - byte)[:, None, :]).reshape(k, n).astype(np.float32)
    by_word = np.ascontiguousarray(scaled.reshape(k // 512, 128, 4, n).transpose(0, 1, 3, 2))
    if fmt == "e4m3":
        words = by_word.astype(ml_dtypes.float8_e4m3fn).view(np.uint8)
    else:
        c = by_word.astype(ml_dtypes.float4_e2m1fn).view(np.uint8) & 0xF
        words = (c[..., 0::2] | (c[..., 1::2] << 4)).reshape(k // 512, 128, 2 * n)
    return np.ascontiguousarray(words), np.ascontiguousarray(byte.astype(np.uint8).reshape(k // 512, 16, n))


def unpack_weight(words, scales, fmt):
    g, _, n = scales.shape
    words = np.ascontiguousarray(words).reshape(g, 128, n, -1)
    if fmt == "e4m3":
        vals = words.view(ml_dtypes.float8_e4m3fn).astype(np.float64)
    else:
        nib = np.empty((g, 128, n, 4), np.uint8)
        nib[..., 0::2] = words & 0xF
        nib[..., 1::2] = words >> 4
        vals = E2M1[nib]
    vals = vals * np.repeat(np.exp2(scales.astype(np.float64) - 127.0), 8, axis=1)[..., None]
    return vals.transpose(0, 1, 3, 2).reshape(g * 512, n)


def planes(y):
    n, m = y.shape
    v = y.astype(np.float32).astype(ml_dtypes.bfloat16).astype(np.float64).reshape(n // 32, 32, m)
    top = np.abs(v).max(1)
    byte = np.clip(np.where(top > 0, np.frexp(top)[1] - 1 + 127 - 7, 1), 1, 254)
    codes = (v * np.exp2(127.0 - byte)[:, None, :]).reshape(n, m).astype(np.float32).astype(ml_dtypes.float8_e4m3fn).view(np.uint8)
    words = codes.reshape(n // 512, 128, 4, m).transpose(0, 1, 3, 2)
    return np.ascontiguousarray(words), np.ascontiguousarray(byte.astype(np.uint8).reshape(n // 512, 16, m))


K, R, M, T = 1536, 512, 1536, 512


def setup_inputs():
    n = np.random.standard_normal
    s = mx_kscale(K)[:, None]
    u = mx_kscale(R)[:, None]
    p_w4 = pack_weight(n((K, M)) / np.sqrt(K) / s, "e2m1")
    return {
        "x": (n((K, T)) * s).astype(np.float32),
        "w4_words": p_w4[0],
        "w4_scales": p_w4[1],
        "down": (n((K, R)) / np.sqrt(K) / s * u.T).astype(np.float32),
        "up": (0.5 * n((R, M)) / np.sqrt(R) / u).astype(np.float32),
        "b": (0.3 * n(1536)).astype(np.float32),
    }


def reference(x, w4_words, w4_scales, down, up, b):
    x_ = mxq(f64(x), 0, "e4m3")
    w4_ = unpack_weight(w4_words, w4_scales, "e2m1")
    down_ = mxq(f64(down), 0, "e4m3")
    up_ = mxq(f64(up), 0, "e4m3")
    h_ = mxq(down_.T @ x_, 0, "e4m3")
    y = w4_.T @ x_ + up_.T @ h_
    out_0 = y + f64(b)[:, None]
    return (out_0,) + planes(out_0)

@@ -1,0 +1,200 @@
+from contextlib import ExitStack
+
+import concourse.mybir as mybir
+
+K, R, M, T = 1536, 512, 1536, 512
+FLOPS = 2 * T * (K * R + K * M + R * M)
+
+F32 = mybir.dt.float32
+BF16 = mybir.dt.bfloat16
+I32 = mybir.dt.int32
+U32 = mybir.dt.uint32
+U8 = mybir.dt.uint8
+FP8X4 = mybir.dt.float8_e4m3fn_x4
+FP4X4 = mybir.dt.float4_e2m1fn_x4
+IDENT = mybir.ActivationFunctionType.Identity
+ADD = mybir.AluOpType.add
+
+P = 128
+G = K // 512
+A = M // 512
+OUT_ROW = 4
+
+
+def tile_mix_lowrank_fm_pl_bias_kernel(tc, x, w4_words, w4_scales, down, up, b, out_0, out_1, out_2):
+    nc = tc.nc
+    with ExitStack() as ctx:
+        sb = ctx.enter_context(tc.tile_pool(name="sb", bufs=1))
+        psum = ctx.enter_context(tc.psum_pool(name="psum", bufs=1))
+        ctx.enter_context(tc.manual_schedule())
+
+        def tiles(name, n, shape, dtype):
+            return [sb.tile(shape, dtype, name="%s%d" % (name, i), align_bytes=256) for i in range(n)]
+
+        w_raw = tiles("w_raw", G, [P, 2 * M], U8)
+        w_dealt = tiles("w_dealt", G, [P, 4, M // 4, 2], U8)
+        s_raw = tiles("s_raw", 1, [P, G, M], U8)[0]
+        s_dealt = tiles("s_dealt", 1, [P, 4, G, M // 4], U8)[0]
+        bias_raw = tiles("bias_raw", 1, [P, A, 8], F32)[0]
+        bias = tiles("bias", 1, [P, A, 4], F32)[0]
+        x_raw = tiles("x_raw", G, [P, 4, 512], F32)
+        d_raw = tiles("d_raw", G, [P, 4, 512], F32)
+        u_raw = tiles("u_raw", A, [P, 4, 512], F32)
+        y_f32 = tiles("y_f32", A, [P, 4, 512], F32)
+        h_rows = tiles("h_rows", 1, [P, 4, 512], BF16)[0]
+
+        def operand(name, n):
+            return list(zip(tiles(name + "_bf", n, [P, 2048], BF16), tiles(name + "_q", n, [P, 512], U32), tiles(name + "_s", n, [P, 512], U8)))
+
+        xq, dq, uq, hq = operand("x", G), operand("d", G), operand("u", A), operand("h", 1)[0]
+        y_bf = tiles("y_bf", A, [P, 2048], BF16)
+        y_q = tiles("y_q", A, [P, 512], U32)
+        y_s = tiles("y_s", 1, [P, A, 512], U8)[0]
+
+        def bank(i):
+            return psum.tile([P, 512], F32, name="bank%d" % i, tag="bank%d" % i)
+
+        def copy(engine, out, in_):
+            if engine == "v":
+                nc.vector.tensor_copy(out=out, in_=in_)
+            else:
+                nc.scalar.copy(out=out, in_=in_)
+
+        def interleave(engine, src, dst, m0, m1):
+            copy(engine,
+                 dst[:, 16 * m0:16 * m1].rearrange("p (m i j) -> p m j i", i=4, j=4),
+                 src[:, :, 4 * m0:4 * m1].rearrange("p j (m i) -> p m j i", i=4))
+
+        def interleave_dealt(engine, src, dst, m0, m1):
+            copy(engine,
+                 dst[:].rearrange("p (i m j) -> p m j i", i=4, j=4)[:, m0:m1],
+                 src[:, :, 4 * m0:4 * m1].rearrange("p j (m i) -> p m j i", i=4))
+
+        def quantize(op, c0=0, c1=512):
+            bf, q, s = op
+            nc.vector.quantize_mx(out=q[:, c0:c1].bitcast(FP8X4), scales=s[:, c0:c1], in_=bf[:, 4 * c0:4 * c1])
+
+        def mm8(acc, stat, r, mov, start, stop):
+            cols = slice(128 * r, 128 * (r + 1))
+            nc.tensor.matmul_mx(out=acc[:], lhsT=stat[1][:, cols].bitcast(FP8X4), lhsT_scale=stat[2][:, cols],
+                                rhs=mov[1][:].bitcast(FP8X4), rhs_scale=mov[2][:], start=start, stop=stop)
+
+        def base(acc, a, r, g):
+            cols = slice(128 * a, 128 * (a + 1))
+            nc.tensor.matmul_mx(out=acc[:], lhsT=w_dealt[g][:, r, cols, :].rearrange("p m b -> p (m b)").bitcast(FP4X4),
+                                lhsT_scale=s_dealt[:, r, g, cols],
+                                rhs=xq[g][1][:].bitcast(FP8X4), rhs_scale=xq[g][2][:], start=(g == 0), stop=False)
+
+        def branch(acc, a, r):
+            mm8(acc, uq[a], r, hq, False, True)
+
+        def deal_words(g):
+            nc.vector.tensor_copy(out=w_dealt[g][:], in_=w_raw[g][:].rearrange("p (m r b) -> p r m b", r=4, b=2))
+
+        def drain(acc, a, r):
+            nc.scalar.activation(out=y_f32[a][:, r, :], in_=acc[:], func=IDENT, bias=bias[:, a, r:r + 1])
+
+        def store_rows(a, r0, r1):
+            rows = out_0[512 * a:512 * (a + 1), :].rearrange("(p r) t -> p r t", r=4)
+            nc.sync.dma_start(out=rows[:, r0:r1, :], in_=y_f32[a][:, r0:r1, :])
+
+        def quantize_y(a, c0=0, c1=512):
+            nc.vector.quantize_mx(out=y_q[a][:, c0:c1].bitcast(FP8X4), scales=y_s[OUT_ROW:P, a, c0:c1], in_=y_bf[a][:, 4 * c0:4 * c1])
+
+        def store_words(a):
+            nc.sync.dma_start(out=out_1[a].rearrange("p t i -> p (t i)").bitcast(I32), in_=y_q[a][:].bitcast(I32))
+
+        def store_scales(queue, a0, a1, q):
+            queue.dma_start(out=out_2[a0:a1, 4 * q:4 * q + 4, :].rearrange("a r t -> r a t").bitcast(I32),
+                            in_=y_s[32 * q + OUT_ROW:32 * q + OUT_ROW + 4, a0:a1, :].bitcast(I32))
+
+        nc.vector.memset(s_raw[:].rearrange("p g n -> p (g n)").bitcast(I32), 0)
+        nc.gpsimd.dma_start(out=bias_raw[:, :, 0:4], in_=b.rearrange("(a p r) -> p a r", a=A, r=4))
+        for g in range(G):
+            nc.sync.dma_start(out=w_raw[g][:].bitcast(I32), in_=w4_words[g].bitcast(I32))
+            nc.sync.dma_start(out=x_raw[g][:], in_=x[512 * g:512 * (g + 1), :].rearrange("(p j) t -> p j t", j=4))
+            if g == 0:
+                for q in range(4):
+                    nc.scalar.dma_start(out=s_raw[32 * q:32 * q + 4].bitcast(I32),
+                                        in_=w4_scales[:, 4 * q:4 * q + 4, :].rearrange("g r n -> r g n").bitcast(I32))
+        for g in range(G):
+            nc.sync.dma_start(out=d_raw[g][:], in_=down[512 * g:512 * (g + 1), :].rearrange("(p j) c -> p j c", j=4))
+        for a in range(A):
+            nc.sync.dma_start(out=u_raw[a][:], in_=up[:, 512 * a:512 * (a + 1)].rearrange("(p j) c -> p j c", j=4))
+        nc.scalar.activation(out=bias[:], in_=bias_raw[:, :, 0:4], func=IDENT)
+
+        y0 = [bank(r) for r in range(4)]
+        hb = [bank(4 + r) for r in range(4)]
+
+        deal_words(0)
+        nc.vector.tensor_copy(out=s_dealt[:], in_=s_raw[:].rearrange("p g (m r) -> p r g m", r=4))
+        for g in range(G):
+            interleave("s", x_raw[g], xq[g][0], 0, 128)
+            if g + 1 < G:
+                deal_words(g + 1)
+            quantize(xq[g])
+            for r in range(4):
+                base(y0[r], 0, r, g)
+        split = 88
+        for g in range(G):
+            interleave_dealt("s", d_raw[g], dq[g][0], split, 128)
+            interleave_dealt("v", d_raw[g], dq[g][0], 0, split)
+            for r in range(4):
+                quantize(dq[g], 128 * r, 128 * (r + 1))
+                mm8(hb[r], dq[g], r, xq[g], g == 0, g == G - 1)
+        for r in range(4):
+            copy("sv"[r % 2], h_rows[:, r, :], hb[r][:])
+        y1 = [bank(4 + r) for r in range(4)]
+        for r in range(4):
+            for g in range(G):
+                base(y1[r], 1, r, g)
+        interleave_dealt("s", u_raw[0], uq[0][0], 0, 128)
+        interleave("v", h_rows, hq[0], 0, 128)
+        quantize(hq)
+        quantize(uq[0])
+        interleave_dealt("s", u_raw[1], uq[1][0], 80, 128)
+        interleave_dealt("v", u_raw[1], uq[1][0], 0, 80)
+        quantize(uq[1])
+        for r in range(4):
+            branch(y0[r], 0, r)
+            drain(y0[r], 0, r)
+        store_rows(0, 0, 2)
+        store_rows(0, 2, 4)
+        interleave_dealt("v", u_raw[2], uq[2][0], 0, 128)
+        y2 = [bank(r) for r in range(4)]
+        for g in range(G):
+            base(y2[0], 2, 0, g)
+        for r in range(4):
+            branch(y1[r], 1, r)
+            drain(y1[r], 1, r)
+        quantize(uq[2])
+        interleave("v", y_f32[0], y_bf[0], 0, 128)
+        quantize_y(0)
+        store_rows(1, 0, 2)
+        store_words(0)
+        store_rows(1, 2, 4)
+        for r in (1, 2):
+            for g in range(G):
+                base(y2[r], 2, r, g)
+        interleave("s", y_f32[1], y_bf[1], 80, 128)
+        interleave("v", y_f32[1], y_bf[1], 0, 80)
+        quantize_y(1)
+        for r in (0, 1):
+            branch(y2[r], 2, r)
+            drain(y2[r], 2, r)
+        store_rows(2, 0, 2)
+        store_words(1)
+        for q in range(4):
+            store_scales(nc.sync, 0, 2, q)
+        for g in range(G):
+            base(y2[3], 2, 3, g)
+        for r in (2, 3):
+            branch(y2[r], 2, r)
+            drain(y2[r], 2, r)
+        store_rows(2, 2, 4)
+        interleave("s", y_f32[2], y_bf[2], 88, 128)
+        interleave("v", y_f32[2], y_bf[2], 0, 88)
+        quantize_y(2)
+        store_words(2)
+        for q in range(4):
+            store_scales(nc.scalar if q % 2 else nc.sync, 2, 3, q)

@@ -35,8 +35,7 @@ def tile_mix_lowrank_fm_pl_bias_kernel(tc, x, w4_words, w4_scales, down, up, b, 
         w_dealt = tiles("w_dealt", G, [P, 4, M // 4, 2], U8)
         s_raw = tiles("s_raw", 1, [P, G, M], U8)[0]
         s_dealt = tiles("s_dealt", 1, [P, 4, G, M // 4], U8)[0]
-        bias_raw = tiles("bias_raw", 1, [P, A, 8], F32)[0]
-        bias = tiles("bias", 1, [P, A, 4], F32)[0]
+        bias = tiles("bias", 1, [P, A, 8], F32)[0]
         x_raw = tiles("x_raw", G, [P, 4, 512], F32)
         d_raw = tiles("d_raw", G, [P, 4, 512], F32)
         u_raw = tiles("u_raw", A, [P, 4, 512], F32)
@@ -108,30 +107,37 @@ def tile_mix_lowrank_fm_pl_bias_kernel(tc, x, w4_words, w4_scales, down, up, b, 
             queue.dma_start(out=out_2[a0:a1, 4 * q:4 * q + 4, :].rearrange("a r t -> r a t").bitcast(I32),
                             in_=y_s[32 * q + OUT_ROW:32 * q + OUT_ROW + 4, a0:a1, :].bitcast(I32))
 
+        def load_rows(dst, rows):
+            nc.sync.dma_start(out=dst[:], in_=rows.rearrange("(p j) c -> p j c", j=4))
+
+        def drain_part(acc, a, r, c0, c1):
+            nc.scalar.activation(out=y_f32[a][:, r, c0:c1], in_=acc[:, c0:c1], func=IDENT, bias=bias[:, a, r:r + 1])
+
         nc.vector.memset(s_raw[:].rearrange("p g n -> p (g n)").bitcast(I32), 0)
-        nc.gpsimd.dma_start(out=bias_raw[:, :, 0:4], in_=b.rearrange("(a p r) -> p a r", a=A, r=4))
         for g in range(G):
             nc.sync.dma_start(out=w_raw[g][:].bitcast(I32), in_=w4_words[g].bitcast(I32))
-            nc.sync.dma_start(out=x_raw[g][:], in_=x[512 * g:512 * (g + 1), :].rearrange("(p j) t -> p j t", j=4))
+            load_rows(x_raw[g], x[512 * g:512 * (g + 1), :])
             if g == 0:
                 for q in range(4):
                     nc.scalar.dma_start(out=s_raw[32 * q:32 * q + 4].bitcast(I32),
                                         in_=w4_scales[:, 4 * q:4 * q + 4, :].rearrange("g r n -> r g n").bitcast(I32))
         for g in range(G):
-            nc.sync.dma_start(out=d_raw[g][:], in_=down[512 * g:512 * (g + 1), :].rearrange("(p j) c -> p j c", j=4))
+            load_rows(d_raw[g], down[512 * g:512 * (g + 1), :])
         for a in range(A):
-            nc.sync.dma_start(out=u_raw[a][:], in_=up[:, 512 * a:512 * (a + 1)].rearrange("(p j) c -> p j c", j=4))
-        nc.scalar.activation(out=bias[:], in_=bias_raw[:, :, 0:4], func=IDENT)
+            load_rows(u_raw[a], up[:, 512 * a:512 * (a + 1)])
+            if a == 0:
+                nc.sync.dma_start(out=bias[:, :, 0:4], in_=b.rearrange("(a p r) -> p a r", a=A, r=4))
 
         y0 = [bank(r) for r in range(4)]
         hb = [bank(4 + r) for r in range(4)]
 
         deal_words(0)
+        deal_words(1)
         nc.vector.tensor_copy(out=s_dealt[:], in_=s_raw[:].rearrange("p g (m r) -> p r g m", r=4))
         for g in range(G):
             interleave("s", x_raw[g], xq[g][0], 0, 128)
-            if g + 1 < G:
-                deal_words(g + 1)
+            if g == 1:
+                deal_words(2)
             quantize(xq[g])
             for r in range(4):
                 base(y0[r], 0, r, g)
@@ -150,51 +156,58 @@ def tile_mix_lowrank_fm_pl_bias_kernel(tc, x, w4_words, w4_scales, down, up, b, 
                 base(y1[r], 1, r, g)
         interleave_dealt("s", u_raw[0], uq[0][0], 0, 128)
         interleave("v", h_rows, hq[0], 0, 128)
+        interleave_dealt("v", u_raw[1], uq[1][0], 0, 32)
         quantize(hq)
-        quantize(uq[0])
-        interleave_dealt("s", u_raw[1], uq[1][0], 80, 128)
-        interleave_dealt("v", u_raw[1], uq[1][0], 0, 80)
-        quantize(uq[1])
+        for r in range(4):
+            quantize(uq[0], 128 * r, 128 * (r + 1))
+        interleave_dealt("s", u_raw[1], uq[1][0], 96, 128)
+        interleave_dealt("v", u_raw[1], uq[1][0], 32, 96)
         for r in range(4):
             branch(y0[r], 0, r)
             drain(y0[r], 0, r)
-        store_rows(0, 0, 2)
-        store_rows(0, 2, 4)
-        interleave_dealt("v", u_raw[2], uq[2][0], 0, 128)
+            store_rows(0, r, r + 1)
+        interleave_dealt("v", u_raw[2], uq[2][0], 0, 32)
+        quantize(uq[1])
+        interleave_dealt("v", u_raw[2], uq[2][0], 32, 128)
         y2 = [bank(r) for r in range(4)]
         for g in range(G):
             base(y2[0], 2, 0, g)
         for r in range(4):
             branch(y1[r], 1, r)
             drain(y1[r], 1, r)
+            if r % 2:
+                store_rows(1, r - 1, r + 1)
+        interleave("v", y_f32[0], y_bf[0], 0, 64)
         quantize(uq[2])
-        interleave("v", y_f32[0], y_bf[0], 0, 128)
+        interleave("v", y_f32[0], y_bf[0], 64, 128)
+        for g in range(G):
+            base(y2[1], 2, 1, g)
+        interleave("v", y_f32[1], y_bf[1], 0, 32)
         quantize_y(0)
-        store_rows(1, 0, 2)
+        interleave("v", y_f32[1], y_bf[1], 32, 128)
         store_words(0)
-        store_rows(1, 2, 4)
-        for r in (1, 2):
-            for g in range(G):
-                base(y2[r], 2, r, g)
-        interleave("s", y_f32[1], y_bf[1], 80, 128)
-        interleave("v", y_f32[1], y_bf[1], 0, 80)
-        quantize_y(1)
         for r in (0, 1):
             branch(y2[r], 2, r)
             drain(y2[r], 2, r)
         store_rows(2, 0, 2)
+        quantize_y(1)
+        for g in range(G):
+            base(y2[2], 2, 2, g)
+        branch(y2[2], 2, 2)
+        drain(y2[2], 2, 2)
+        store_rows(2, 2, 3)
         store_words(1)
-        for q in range(4):
-            store_scales(nc.sync, 0, 2, q)
         for g in range(G):
             base(y2[3], 2, 3, g)
-        for r in (2, 3):
-            branch(y2[r], 2, r)
-            drain(y2[r], 2, r)
-        store_rows(2, 2, 4)
-        interleave("s", y_f32[2], y_bf[2], 88, 128)
-        interleave("v", y_f32[2], y_bf[2], 0, 88)
-        quantize_y(2)
+        branch(y2[3], 2, 3)
+        drain_part(y2[3], 2, 3, 0, 256)
+        drain_part(y2[3], 2, 3, 256, 512)
+        store_rows(2, 3, 4)
+        interleave("v", y_f32[2], y_bf[2], 0, 64)
+        interleave("s", y_f32[2], y_bf[2], 96, 128)
+        interleave("v", y_f32[2], y_bf[2], 64, 96)
+        quantize_y(2, 0, 256)
+        quantize_y(2, 256, 512)
         store_words(2)
         for q in range(4):
-            store_scales(nc.scalar if q % 2 else nc.sync, 2, 3, q)
+            store_scales(nc.scalar if q % 2 else nc.sync, 0, 3, q)

@@ -19,6 +19,7 @@ P = 128
 G = K // 512
 A = M // 512
 OUT_ROW = 4
+EARLY = 2
 
 
 def tile_mix_lowrank_fm_pl_bias_kernel(tc, x, w4_words, w4_scales, down, up, b, out_0, out_1, out_2):
@@ -31,12 +32,13 @@ def tile_mix_lowrank_fm_pl_bias_kernel(tc, x, w4_words, w4_scales, down, up, b, 
         def tiles(name, n, shape, dtype):
             return [sb.tile(shape, dtype, name="%s%d" % (name, i), align_bytes=256) for i in range(n)]
 
-        w_raw = tiles("w_raw", G, [P, 2 * M], U8)
-        w_dealt = tiles("w_dealt", G, [P, 4, M // 4, 2], U8)
+        w_raw = [tiles("w_raw_early", 1, [P, G, 1024 * EARLY], U8)[0], tiles("w_raw_late", 1, [P, G, 1024], U8)[0]]
+        w_dealt = [tiles("w_early", G, [P, 4, 128 * EARLY, 2], U8), tiles("w_late", G, [P, 4, 128, 2], U8)]
         s_raw = tiles("s_raw", 1, [P, G, M], U8)[0]
         s_dealt = tiles("s_dealt", 1, [P, 4, G, M // 4], U8)[0]
         bias = tiles("bias", 1, [P, A, 8], F32)[0]
-        x_raw = tiles("x_raw", G, [P, 4, 512], F32)
+        x_all = tiles("x_all", 1, [P, G, 4, 512], F32)[0]
+        x_raw = [x_all[:, g] for g in range(G)]
         d_raw = tiles("d_raw", G, [P, 4, 512], F32)
         u_raw = tiles("u_raw", A, [P, 4, 512], F32)
         y_f32 = tiles("y_f32", A, [P, 4, 512], F32)
@@ -47,7 +49,8 @@ def tile_mix_lowrank_fm_pl_bias_kernel(tc, x, w4_words, w4_scales, down, up, b, 
 
         xq, dq, uq, hq = operand("x", G), operand("d", G), operand("u", A), operand("h", 1)[0]
         y_bf = tiles("y_bf", A, [P, 2048], BF16)
-        y_q = tiles("y_q", A, [P, 512], U32)
+        y_q_all = tiles("y_q", 1, [P, A, 512], U32)[0]
+        y_q = [y_q_all[:, a] for a in range(A)]
         y_s = tiles("y_s", 1, [P, A, 512], U8)[0]
 
         def bank(i):
@@ -64,10 +67,10 @@ def tile_mix_lowrank_fm_pl_bias_kernel(tc, x, w4_words, w4_scales, down, up, b, 
                  dst[:, 16 * m0:16 * m1].rearrange("p (m i j) -> p m j i", i=4, j=4),
                  src[:, :, 4 * m0:4 * m1].rearrange("p j (m i) -> p m j i", i=4))
 
-        def interleave_dealt(engine, src, dst, m0, m1):
+        def interleave_dealt(engine, src, dst, i0, i1):
             copy(engine,
-                 dst[:].rearrange("p (i m j) -> p m j i", i=4, j=4)[:, m0:m1],
-                 src[:, :, 4 * m0:4 * m1].rearrange("p j (m i) -> p m j i", i=4))
+                 dst[:, 512 * i0:512 * i1].rearrange("p (i m j) -> p m j i", m=128, j=4),
+                 src[:].rearrange("p j (m i) -> p m j i", i=4)[:, :, :, i0:i1])
 
         def quantize(op, c0=0, c1=512):
             bf, q, s = op
@@ -80,15 +83,50 @@ def tile_mix_lowrank_fm_pl_bias_kernel(tc, x, w4_words, w4_scales, down, up, b, 
 
         def base(acc, a, r, g):
             cols = slice(128 * a, 128 * (a + 1))
-            nc.tensor.matmul_mx(out=acc[:], lhsT=w_dealt[g][:, r, cols, :].rearrange("p m b -> p (m b)").bitcast(FP4X4),
+            nc.tensor.matmul_mx(out=acc[:], lhsT=w_tile(a, r, g),
                                 lhsT_scale=s_dealt[:, r, g, cols],
                                 rhs=xq[g][1][:].bitcast(FP8X4), rhs_scale=xq[g][2][:], start=(g == 0), stop=False)
 
         def branch(acc, a, r):
             mm8(acc, uq[a], r, hq, False, True)
 
-        def deal_words(g):
-            nc.vector.tensor_copy(out=w_dealt[g][:], in_=w_raw[g][:].rearrange("p (m r b) -> p r m b", r=4, b=2))
+        def deal_words(part, g):
+            nc.vector.tensor_copy(out=w_dealt[part][g][:], in_=w_raw[part][:, g].rearrange("p (m r b) -> p r m b", r=4, b=2))
+
+        def w_tile(a, r, g):
+            part, m0 = (0, 128 * a) if a < EARLY else (1, 0)
+            return w_dealt[part][g][:, r, m0:m0 + 128, :].rearrange("p m b -> p (m b)").bitcast(FP4X4)
+
+        def deal_scales(a0, a1):
+            nc.vector.tensor_copy(out=s_dealt[:, :, :, 128 * a0:128 * a1],
+                                  in_=s_raw[:, :, 512 * a0:512 * a1].rearrange("p g (m r) -> p r g m", r=4))
+
+        def load_words(part, g0, g1):
+            c0, c1 = (0, 1024 * EARLY) if part == 0 else (1024 * EARLY, 1024 * A)
+            nc.sync.dma_start(out=w_raw[part][:, g0:g1].bitcast(I32),
+                              in_=w4_words[g0:g1, :, c0:c1].rearrange("g p c -> p g c").bitcast(I32))
+
+        def load_scales(queue, a0, a1):
+            for q in range(4):
+                queue.dma_start(out=s_raw[32 * q:32 * q + 4, :, 512 * a0:512 * a1].bitcast(I32),
+                                in_=w4_scales[:, 4 * q:4 * q + 4, 512 * a0:512 * a1].rearrange("g r n -> r g n").bitcast(I32))
+
+        def load_rows(dst, rows):
+            nc.sync.dma_start(out=dst[:], in_=rows.rearrange("(p j) c -> p j c", j=4))
+
+        def narrow_group(acc, a, r, c0):
+            cols, ts = slice(128 * a, 128 * (a + 1)), slice(c0, c0 + 128)
+            for g in range(G):
+                nc.tensor.matmul_mx(out=acc[:, 0:128], lhsT=w_tile(a, r, g),
+                                    lhsT_scale=s_dealt[:, r, g, cols],
+                                    rhs=xq[g][1][:, ts].bitcast(FP8X4), rhs_scale=xq[g][2][:, ts], start=(g == 0), stop=False)
+            cols = slice(128 * r, 128 * (r + 1))
+            nc.tensor.matmul_mx(out=acc[:, 0:128], lhsT=uq[a][1][:, cols].bitcast(FP8X4), lhsT_scale=uq[a][2][:, cols],
+                                rhs=hq[1][:, ts].bitcast(FP8X4), rhs_scale=hq[2][:, ts], start=False, stop=True)
+            nc.scalar.activation(out=y_f32[a][:, r, ts], in_=acc[:, 0:128], func=IDENT, bias=bias[:, a, r:r + 1])
+
+        def drain_v(acc, a, r):
+            nc.vector.tensor_scalar(out=y_f32[a][:, r, :], in0=acc[:], scalar1=bias[:, a, r:r + 1], scalar2=None, op0=ADD)
 
         def drain(acc, a, r):
             nc.scalar.activation(out=y_f32[a][:, r, :], in_=acc[:], func=IDENT, bias=bias[:, a, r:r + 1])
@@ -100,96 +138,90 @@ def tile_mix_lowrank_fm_pl_bias_kernel(tc, x, w4_words, w4_scales, down, up, b, 
         def quantize_y(a, c0=0, c1=512):
             nc.vector.quantize_mx(out=y_q[a][:, c0:c1].bitcast(FP8X4), scales=y_s[OUT_ROW:P, a, c0:c1], in_=y_bf[a][:, 4 * c0:4 * c1])
 
-        def store_words(a):
-            nc.sync.dma_start(out=out_1[a].rearrange("p t i -> p (t i)").bitcast(I32), in_=y_q[a][:].bitcast(I32))
+        def store_words(a, c0=0, c1=512):
+            nc.sync.dma_start(out=out_1[a, :, c0:c1, :].rearrange("p t i -> p (t i)").bitcast(I32), in_=y_q[a][:, c0:c1].bitcast(I32))
+
+        def store_words_of(a0, a1):
+            nc.sync.dma_start(out=out_1[a0:a1].rearrange("a p t i -> p a (t i)").bitcast(I32), in_=y_q_all[:, a0:a1].bitcast(I32))
 
         def store_scales(queue, a0, a1, q):
             queue.dma_start(out=out_2[a0:a1, 4 * q:4 * q + 4, :].rearrange("a r t -> r a t").bitcast(I32),
                             in_=y_s[32 * q + OUT_ROW:32 * q + OUT_ROW + 4, a0:a1, :].bitcast(I32))
 
-        def load_rows(dst, rows):
-            nc.sync.dma_start(out=dst[:], in_=rows.rearrange("(p j) c -> p j c", j=4))
-
-        def drain_part(acc, a, r, c0, c1):
-            nc.scalar.activation(out=y_f32[a][:, r, c0:c1], in_=acc[:, c0:c1], func=IDENT, bias=bias[:, a, r:r + 1])
-
         nc.vector.memset(s_raw[:].rearrange("p g n -> p (g n)").bitcast(I32), 0)
+        load_words(0, 0, G)
+        load_scales(nc.sync, 0, 3)
         for g in range(G):
-            nc.sync.dma_start(out=w_raw[g][:].bitcast(I32), in_=w4_words[g].bitcast(I32))
             load_rows(x_raw[g], x[512 * g:512 * (g + 1), :])
-            if g == 0:
-                for q in range(4):
-                    nc.scalar.dma_start(out=s_raw[32 * q:32 * q + 4].bitcast(I32),
-                                        in_=w4_scales[:, 4 * q:4 * q + 4, :].rearrange("g r n -> r g n").bitcast(I32))
         for g in range(G):
             load_rows(d_raw[g], down[512 * g:512 * (g + 1), :])
-        for a in range(A):
-            load_rows(u_raw[a], up[:, 512 * a:512 * (a + 1)])
-            if a == 0:
-                nc.sync.dma_start(out=bias[:, :, 0:4], in_=b.rearrange("(a p r) -> p a r", a=A, r=4))
+        load_rows(u_raw[0], up[:, 0:512])
+        load_rows(u_raw[1], up[:, 512:1024])
+        nc.sync.dma_start(out=bias[:, :, 0:4], in_=b.rearrange("(a p r) -> p a r", a=A, r=4))
+        load_words(1, 0, G)
+        load_rows(u_raw[2], up[:, 1024:1536])
 
         y0 = [bank(r) for r in range(4)]
         hb = [bank(4 + r) for r in range(4)]
 
-        deal_words(0)
-        deal_words(1)
-        nc.vector.tensor_copy(out=s_dealt[:], in_=s_raw[:].rearrange("p g (m r) -> p r g m", r=4))
+        for g in range(G):
+            deal_words(0, g)
+        deal_scales(0, 3)
         for g in range(G):
             interleave("s", x_raw[g], xq[g][0], 0, 128)
-            if g == 1:
-                deal_words(2)
             quantize(xq[g])
             for r in range(4):
                 base(y0[r], 0, r, g)
-        split = 88
         for g in range(G):
-            interleave_dealt("s", d_raw[g], dq[g][0], split, 128)
-            interleave_dealt("v", d_raw[g], dq[g][0], 0, split)
+            interleave_dealt("s", d_raw[g], dq[g][0], 2, 4)
+            interleave_dealt("v", d_raw[g], dq[g][0], 0, 2)
             for r in range(4):
                 quantize(dq[g], 128 * r, 128 * (r + 1))
                 mm8(hb[r], dq[g], r, xq[g], g == 0, g == G - 1)
         for r in range(4):
-            copy("sv"[r % 2], h_rows[:, r, :], hb[r][:])
+            copy("svss"[r], h_rows[:, r, :], hb[r][:])
         y1 = [bank(4 + r) for r in range(4)]
         for r in range(4):
             for g in range(G):
                 base(y1[r], 1, r, g)
-        interleave_dealt("s", u_raw[0], uq[0][0], 0, 128)
-        interleave("v", h_rows, hq[0], 0, 128)
-        interleave_dealt("v", u_raw[1], uq[1][0], 0, 32)
+        interleave_dealt("v", u_raw[0], uq[0][0], 0, 4)
+        interleave("s", h_rows, hq[0], 72, 128)
+        interleave("v", h_rows, hq[0], 0, 72)
+        quantize(uq[0], 0, 256)
         quantize(hq)
-        for r in range(4):
-            quantize(uq[0], 128 * r, 128 * (r + 1))
-        interleave_dealt("s", u_raw[1], uq[1][0], 96, 128)
-        interleave_dealt("v", u_raw[1], uq[1][0], 32, 96)
+        quantize(uq[0], 256, 512)
+        interleave_dealt("s", u_raw[1], uq[1][0], 2, 4)
+        interleave_dealt("v", u_raw[1], uq[1][0], 0, 2)
+        deal_words(1, 0)
         for r in range(4):
             branch(y0[r], 0, r)
             drain(y0[r], 0, r)
             store_rows(0, r, r + 1)
-        interleave_dealt("v", u_raw[2], uq[2][0], 0, 32)
         quantize(uq[1])
-        interleave_dealt("v", u_raw[2], uq[2][0], 32, 128)
-        y2 = [bank(r) for r in range(4)]
-        for g in range(G):
-            base(y2[0], 2, 0, g)
+        deal_words(1, 1)
+        deal_words(1, 2)
+        y2 = [bank(r) for r in range(3)]
         for r in range(4):
             branch(y1[r], 1, r)
             drain(y1[r], 1, r)
             if r % 2:
                 store_rows(1, r - 1, r + 1)
-        interleave("v", y_f32[0], y_bf[0], 0, 64)
-        quantize(uq[2])
-        interleave("v", y_f32[0], y_bf[0], 64, 128)
-        for g in range(G):
-            base(y2[1], 2, 1, g)
-        interleave("v", y_f32[1], y_bf[1], 0, 32)
+        interleave_dealt("v", u_raw[2], uq[2][0], 0, 2)
+        interleave_dealt("v", u_raw[2], uq[2][0], 2, 4)
+        quantize(uq[2], 0, 256)
+        interleave("v", y_f32[0], y_bf[0], 0, 128)
+        quantize(uq[2], 256, 512)
+        for r in range(0, 2):
+            for g in range(G):
+                base(y2[r], 2, r, g)
         quantize_y(0)
-        interleave("v", y_f32[1], y_bf[1], 32, 128)
-        store_words(0)
         for r in (0, 1):
             branch(y2[r], 2, r)
             drain(y2[r], 2, r)
         store_rows(2, 0, 2)
+        store_words(0)
+        interleave("s", y_f32[1], y_bf[1], 88, 128)
+        interleave("v", y_f32[1], y_bf[1], 0, 88)
         quantize_y(1)
         for g in range(G):
             base(y2[2], 2, 2, g)
@@ -197,16 +229,15 @@ def tile_mix_lowrank_fm_pl_bias_kernel(tc, x, w4_words, w4_scales, down, up, b, 
         drain(y2[2], 2, 2)
         store_rows(2, 2, 3)
         store_words(1)
-        for g in range(G):
-            base(y2[3], 2, 3, g)
-        branch(y2[3], 2, 3)
-        drain_part(y2[3], 2, 3, 0, 256)
-        drain_part(y2[3], 2, 3, 256, 512)
+        for c in range(4):
+            narrow_group(bank(4 + c), 2, 3, 128 * c)
         store_rows(2, 3, 4)
-        interleave("v", y_f32[2], y_bf[2], 0, 64)
+        interleave("v", y_f32[2], y_bf[2], 0, 32)
+        interleave("v", y_f32[2], y_bf[2], 32, 64)
         interleave("s", y_f32[2], y_bf[2], 96, 128)
+        quantize_y(2, 0, 128)
         interleave("v", y_f32[2], y_bf[2], 64, 96)
-        quantize_y(2, 0, 256)
+        quantize_y(2, 128, 256)
         quantize_y(2, 256, 512)
         store_words(2)
         for q in range(4):

@@ -62,10 +62,10 @@ def tile_mix_lowrank_fm_pl_bias_kernel(tc, x, w4_words, w4_scales, down, up, b, 
             else:
                 nc.scalar.copy(out=out, in_=in_)
 
-        def interleave(engine, src, dst, m0, m1):
+        def interleave(engine, src, dst, m0, m1, run=2):
             copy(engine,
-                 dst[:, 16 * m0:16 * m1].rearrange("p (m i j) -> p m j i", i=4, j=4),
-                 src[:, :, 4 * m0:4 * m1].rearrange("p j (m i) -> p m j i", i=4))
+                 dst[:, 16 * m0:16 * m1].rearrange("p (m i j) -> p m j i", i=run, j=4),
+                 src[:, :, 4 * m0:4 * m1].rearrange("p j (m i) -> p m j i", i=run))
 
         def interleave_dealt(engine, src, dst, i0, i1):
             copy(engine,
@@ -107,9 +107,9 @@ def tile_mix_lowrank_fm_pl_bias_kernel(tc, x, w4_words, w4_scales, down, up, b, 
                               in_=w4_words[g0:g1, :, c0:c1].rearrange("g p c -> p g c").bitcast(I32))
 
         def load_scales(queue, a0, a1):
-            for q in range(4):
-                queue.dma_start(out=s_raw[32 * q:32 * q + 4, :, 512 * a0:512 * a1].bitcast(I32),
-                                in_=w4_scales[:, 4 * q:4 * q + 4, 512 * a0:512 * a1].rearrange("g r n -> r g n").bitcast(I32))
+            for r in range(4):
+                queue.dma_start(out=s_raw[r:P:32, :, 512 * a0:512 * a1].bitcast(I32),
+                                in_=w4_scales[:, r:16:4, 512 * a0:512 * a1].rearrange("g q n -> q g n").bitcast(I32))
 
         def load_rows(dst, rows):
             nc.sync.dma_start(out=dst[:], in_=rows.rearrange("(p j) c -> p j c", j=4))
@@ -144,9 +144,9 @@ def tile_mix_lowrank_fm_pl_bias_kernel(tc, x, w4_words, w4_scales, down, up, b, 
         def store_words_of(a0, a1):
             nc.sync.dma_start(out=out_1[a0:a1].rearrange("a p t i -> p a (t i)").bitcast(I32), in_=y_q_all[:, a0:a1].bitcast(I32))
 
-        def store_scales(queue, a0, a1, q):
-            queue.dma_start(out=out_2[a0:a1, 4 * q:4 * q + 4, :].rearrange("a r t -> r a t").bitcast(I32),
-                            in_=y_s[32 * q + OUT_ROW:32 * q + OUT_ROW + 4, a0:a1, :].bitcast(I32))
+        def store_scales(queue, a0, a1, r):
+            queue.dma_start(out=out_2[a0:a1, r:16:4, :].rearrange("a q t -> q a t").bitcast(I32),
+                            in_=y_s[OUT_ROW + r:P:32, a0:a1, :].bitcast(I32))
 
         nc.vector.memset(s_raw[:].rearrange("p g n -> p (g n)").bitcast(I32), 0)
         load_words(0, 0, G)
@@ -184,9 +184,10 @@ def tile_mix_lowrank_fm_pl_bias_kernel(tc, x, w4_words, w4_scales, down, up, b, 
         for r in range(4):
             for g in range(G):
                 base(y1[r], 1, r, g)
-        interleave_dealt("v", u_raw[0], uq[0][0], 0, 4)
-        interleave("s", h_rows, hq[0], 72, 128)
-        interleave("v", h_rows, hq[0], 0, 72)
+        interleave_dealt("v", u_raw[0], uq[0][0], 0, 2)
+        interleave_dealt("v", u_raw[0], uq[0][0], 2, 4)
+        interleave("s", h_rows, hq[0], 72, 128, 4)
+        interleave("v", h_rows, hq[0], 0, 72, 4)
         quantize(uq[0], 0, 256)
         quantize(hq)
         quantize(uq[0], 256, 512)

@@ -9,6 +9,7 @@ F32 = mybir.dt.float32
 BF16 = mybir.dt.bfloat16
 I32 = mybir.dt.int32
 U32 = mybir.dt.uint32
+U16 = mybir.dt.uint16
 U8 = mybir.dt.uint8
 FP8X4 = mybir.dt.float8_e4m3fn_x4
 FP4X4 = mybir.dt.float4_e2m1fn_x4
@@ -19,7 +20,6 @@ P = 128
 G = K // 512
 A = M // 512
 OUT_ROW = 4
-EARLY = 2
 
 
 def tile_mix_lowrank_fm_pl_bias_kernel(tc, x, w4_words, w4_scales, down, up, b, out_0, out_1, out_2):
@@ -32,8 +32,8 @@ def tile_mix_lowrank_fm_pl_bias_kernel(tc, x, w4_words, w4_scales, down, up, b, 
         def tiles(name, n, shape, dtype):
             return [sb.tile(shape, dtype, name="%s%d" % (name, i), align_bytes=256) for i in range(n)]
 
-        w_raw = [tiles("w_raw_early", 1, [P, G, 1024 * EARLY], U8)[0], tiles("w_raw_late", 1, [P, G, 1024], U8)[0]]
-        w_dealt = [tiles("w_early", G, [P, 4, 128 * EARLY, 2], U8), tiles("w_late", G, [P, 4, 128, 2], U8)]
+        w_raw = tiles("w_raw", A, [P, G, 1024], U8)
+        w_dealt = [tiles("w_dealt%d_" % a, G, [P, 4, 256], U8) for a in range(A)]
         s_raw = tiles("s_raw", 1, [P, G, M], U8)[0]
         s_dealt = tiles("s_dealt", 1, [P, 4, G, M // 4], U8)[0]
         bias = tiles("bias", 1, [P, A, 8], F32)[0]
@@ -42,7 +42,6 @@ def tile_mix_lowrank_fm_pl_bias_kernel(tc, x, w4_words, w4_scales, down, up, b, 
         d_raw = tiles("d_raw", G, [P, 4, 512], F32)
         u_raw = tiles("u_raw", A, [P, 4, 512], F32)
         y_f32 = tiles("y_f32", A, [P, 4, 512], F32)
-        h_rows = tiles("h_rows", 1, [P, 4, 512], BF16)[0]
 
         def operand(name, n):
             return list(zip(tiles(name + "_bf", n, [P, 2048], BF16), tiles(name + "_q", n, [P, 512], U32), tiles(name + "_s", n, [P, 512], U8)))
@@ -67,10 +66,19 @@ def tile_mix_lowrank_fm_pl_bias_kernel(tc, x, w4_words, w4_scales, down, up, b, 
                  dst[:, 16 * m0:16 * m1].rearrange("p (m i j) -> p m j i", i=run, j=4),
                  src[:, :, 4 * m0:4 * m1].rearrange("p j (m i) -> p m j i", i=run))
 
-        def interleave_dealt(engine, src, dst, i0, i1):
+        def interleave_dealt(engine, src, dst, i0, i1, m0=0, m1=128):
             copy(engine,
-                 dst[:, 512 * i0:512 * i1].rearrange("p (i m j) -> p m j i", m=128, j=4),
-                 src[:].rearrange("p j (m i) -> p m j i", i=4)[:, :, :, i0:i1])
+                 dst[:, 512 * i0:512 * i1].rearrange("p (i m j) -> p m j i", m=128, j=4)[:, m0:m1],
+                 src[:].rearrange("p j (m i) -> p m j i", i=4)[:, m0:m1, :, i0:i1])
+
+        def h_pass(g, j, c):
+            cols, ts = slice(128 * j, 128 * (j + 1)), slice(128 * c, 128 * (c + 1))
+            nc.tensor.matmul_mx(out=hb[c][:, cols], lhsT=dq[g][1][:, cols].bitcast(FP8X4), lhsT_scale=dq[g][2][:, cols],
+                                rhs=xq[g][1][:, ts].bitcast(FP8X4), rhs_scale=xq[g][2][:, ts],
+                                start=(g == 0 and j == 0), stop=(g == G - 1 and j == 3))
+
+        def h_out(engine, c):
+            copy(engine, hq[0][:, 512 * c:512 * (c + 1)].rearrange("p (t j) -> p t j", j=4), hb[c][:].rearrange("p (j t) -> p t j", j=4))
 
         def quantize(op, c0=0, c1=512):
             bf, q, s = op
@@ -90,21 +98,20 @@ def tile_mix_lowrank_fm_pl_bias_kernel(tc, x, w4_words, w4_scales, down, up, b, 
         def branch(acc, a, r):
             mm8(acc, uq[a], r, hq, False, True)
 
-        def deal_words(part, g):
-            nc.vector.tensor_copy(out=w_dealt[part][g][:], in_=w_raw[part][:, g].rearrange("p (m r b) -> p r m b", r=4, b=2))
+        def deal_words(a, g):
+            nc.vector.tensor_copy(out=w_dealt[a][g][:].bitcast(U16),
+                                  in_=w_raw[a][:, g].bitcast(U16).rearrange("p (m r) -> p r m", r=4))
 
         def w_tile(a, r, g):
-            part, m0 = (0, 128 * a) if a < EARLY else (1, 0)
-            return w_dealt[part][g][:, r, m0:m0 + 128, :].rearrange("p m b -> p (m b)").bitcast(FP4X4)
+            return w_dealt[a][g][:, r].bitcast(FP4X4)
 
         def deal_scales(a0, a1):
             nc.vector.tensor_copy(out=s_dealt[:, :, :, 128 * a0:128 * a1],
                                   in_=s_raw[:, :, 512 * a0:512 * a1].rearrange("p g (m r) -> p r g m", r=4))
 
-        def load_words(part, g0, g1):
-            c0, c1 = (0, 1024 * EARLY) if part == 0 else (1024 * EARLY, 1024 * A)
-            nc.sync.dma_start(out=w_raw[part][:, g0:g1].bitcast(I32),
-                              in_=w4_words[g0:g1, :, c0:c1].rearrange("g p c -> p g c").bitcast(I32))
+        def load_words(a):
+            nc.sync.dma_start(out=w_raw[a][:].bitcast(I32),
+                              in_=w4_words[:, :, 1024 * a:1024 * (a + 1)].rearrange("g p c -> p g c").bitcast(I32))
 
         def load_scales(queue, a0, a1):
             for r in range(4):
@@ -149,97 +156,119 @@ def tile_mix_lowrank_fm_pl_bias_kernel(tc, x, w4_words, w4_scales, down, up, b, 
                             in_=y_s[OUT_ROW + r:P:32, a0:a1, :].bitcast(I32))
 
         nc.vector.memset(s_raw[:].rearrange("p g n -> p (g n)").bitcast(I32), 0)
-        load_words(0, 0, G)
+        load_words(0)
         load_scales(nc.sync, 0, 3)
-        for g in range(G):
-            load_rows(x_raw[g], x[512 * g:512 * (g + 1), :])
+        nc.sync.dma_start(out=x_all[:, 0:2], in_=x[0:1024, :].rearrange("(g p j) c -> p g j c", g=2, j=4))
+        load_rows(x_raw[2], x[1024:1536, :])
         for g in range(G):
             load_rows(d_raw[g], down[512 * g:512 * (g + 1), :])
+        load_words(1)
         load_rows(u_raw[0], up[:, 0:512])
-        load_rows(u_raw[1], up[:, 512:1024])
         nc.sync.dma_start(out=bias[:, :, 0:4], in_=b.rearrange("(a p r) -> p a r", a=A, r=4))
-        load_words(1, 0, G)
+        load_rows(u_raw[1], up[:, 512:1024])
+        load_words(2)
         load_rows(u_raw[2], up[:, 1024:1536])
 
         y0 = [bank(r) for r in range(4)]
-        hb = [bank(4 + r) for r in range(4)]
+        hb = [bank(4 + c) for c in range(4)]
 
         for g in range(G):
             deal_words(0, g)
         deal_scales(0, 3)
         for g in range(G):
-            interleave("s", x_raw[g], xq[g][0], 0, 128)
-            quantize(xq[g])
+            interleave("s", x_raw[g], xq[g][0], 64, 128)
+            interleave("v", x_raw[g], xq[g][0], 0, 64)
+            if g:
+                quantize(xq[g - 1])
+        quantize(xq[G - 1])
+        for g in range(G):
             for r in range(4):
                 base(y0[r], 0, r, g)
         for g in range(G):
-            interleave_dealt("s", d_raw[g], dq[g][0], 2, 4)
+            interleave_dealt("s", d_raw[g], dq[g][0], 2, 4, 0, 80)
             interleave_dealt("v", d_raw[g], dq[g][0], 0, 2)
-            for r in range(4):
-                quantize(dq[g], 128 * r, 128 * (r + 1))
-                mm8(hb[r], dq[g], r, xq[g], g == 0, g == G - 1)
-        for r in range(4):
-            copy("svss"[r], h_rows[:, r, :], hb[r][:])
+            interleave_dealt("v", d_raw[g], dq[g][0], 2, 4, 80, 128)
+            for j in range(4):
+                quantize(dq[g], 128 * j, 128 * (j + 1))
+            for j in range(2):
+                for c in range(4):
+                    h_pass(g, j, c)
+            for c in range(4):
+                for j in range(2, 4):
+                    h_pass(g, j, c)
+        for g in range(G):
+            deal_words(1, g)
+        h_out("s", 0)
+        h_out("v", 1)
+        h_out("s", 2)
+        h_out("s", 3)
         y1 = [bank(4 + r) for r in range(4)]
-        for r in range(4):
+        interleave_dealt("v", u_raw[0], uq[0][0], 0, 2)
+        quantize(hq, 0, 256)
+        interleave_dealt("s", u_raw[0], uq[0][0], 2, 4, 0, 48)
+        interleave_dealt("v", u_raw[0], uq[0][0], 2, 4, 48, 128)
+        quantize(uq[0], 0, 256)
+        quantize(hq, 256, 512)
+        quantize(uq[0], 256, 512)
+        for r in range(2):
             for g in range(G):
                 base(y1[r], 1, r, g)
-        interleave_dealt("v", u_raw[0], uq[0][0], 0, 2)
-        interleave_dealt("v", u_raw[0], uq[0][0], 2, 4)
-        interleave("s", h_rows, hq[0], 72, 128, 4)
-        interleave("v", h_rows, hq[0], 0, 72, 4)
-        quantize(uq[0], 0, 256)
-        quantize(hq)
-        quantize(uq[0], 256, 512)
-        interleave_dealt("s", u_raw[1], uq[1][0], 2, 4)
         interleave_dealt("v", u_raw[1], uq[1][0], 0, 2)
-        deal_words(1, 0)
+        interleave_dealt("v", u_raw[1], uq[1][0], 2, 4)
         for r in range(4):
             branch(y0[r], 0, r)
             drain(y0[r], 0, r)
-            store_rows(0, r, r + 1)
-        quantize(uq[1])
-        deal_words(1, 1)
-        deal_words(1, 2)
-        y2 = [bank(r) for r in range(3)]
+            if r % 2:
+                store_rows(0, r - 1, r + 1)
+        quantize(uq[1], 0, 256)
+        deal_words(2, 0)
+        quantize(uq[1], 256, 512)
+        deal_words(2, 1)
+        deal_words(2, 2)
+        for r in range(2, 4):
+            for g in range(G):
+                base(y1[r], 1, r, g)
         for r in range(4):
             branch(y1[r], 1, r)
             drain(y1[r], 1, r)
             if r % 2:
                 store_rows(1, r - 1, r + 1)
+        y2 = [bank(r) for r in range(3)]
+        interleave("v", y_f32[0], y_bf[0], 0, 64)
         interleave_dealt("v", u_raw[2], uq[2][0], 0, 2)
-        interleave_dealt("v", u_raw[2], uq[2][0], 2, 4)
+        interleave("v", y_f32[0], y_bf[0], 64, 128)
         quantize(uq[2], 0, 256)
-        interleave("v", y_f32[0], y_bf[0], 0, 128)
+        quantize_y(0)
+        interleave_dealt("v", u_raw[2], uq[2][0], 2, 4)
+        store_words(0)
+        interleave("v", y_f32[1], y_bf[1], 0, 32)
         quantize(uq[2], 256, 512)
-        for r in range(0, 2):
+        interleave("v", y_f32[1], y_bf[1], 32, 96)
+        for r in range(2):
             for g in range(G):
                 base(y2[r], 2, r, g)
-        quantize_y(0)
-        for r in (0, 1):
+        interleave("s", y_f32[1], y_bf[1], 96, 128)
+        for r in range(2):
             branch(y2[r], 2, r)
             drain(y2[r], 2, r)
         store_rows(2, 0, 2)
-        store_words(0)
-        interleave("s", y_f32[1], y_bf[1], 88, 128)
-        interleave("v", y_f32[1], y_bf[1], 0, 88)
         quantize_y(1)
+        store_words(1)
         for g in range(G):
             base(y2[2], 2, 2, g)
         branch(y2[2], 2, 2)
         drain(y2[2], 2, 2)
-        store_rows(2, 2, 3)
-        store_words(1)
         for c in range(4):
             narrow_group(bank(4 + c), 2, 3, 128 * c)
-        store_rows(2, 3, 4)
+        store_rows(2, 2, 4)
         interleave("v", y_f32[2], y_bf[2], 0, 32)
         interleave("v", y_f32[2], y_bf[2], 32, 64)
-        interleave("s", y_f32[2], y_bf[2], 96, 128)
         quantize_y(2, 0, 128)
-        interleave("v", y_f32[2], y_bf[2], 64, 96)
+        interleave("s", y_f32[2], y_bf[2], 104, 128)
+        interleave("v", y_f32[2], y_bf[2], 64, 104)
         quantize_y(2, 128, 256)
-        quantize_y(2, 256, 512)
+        quantize_y(2, 256, 384)
+        quantize_y(2, 384, 512)
         store_words(2)
         for q in range(4):
             store_scales(nc.scalar if q % 2 else nc.sync, 0, 3, q)

@@ -20,6 +20,7 @@ P = 128
 G = K // 512
 A = M // 512
 OUT_ROW = 4
+BIAS_ROW = 8
 
 
 def tile_mix_lowrank_fm_pl_bias_kernel(tc, x, w4_words, w4_scales, down, up, b, out_0, out_1, out_2):
@@ -36,7 +37,9 @@ def tile_mix_lowrank_fm_pl_bias_kernel(tc, x, w4_words, w4_scales, down, up, b, 
         w_dealt = [tiles("w_dealt%d_" % a, G, [P, 4, 256], U8) for a in range(A)]
         s_raw = tiles("s_raw", 1, [P, G, M], U8)[0]
         s_dealt = tiles("s_dealt", 1, [P, 4, G, M // 4], U8)[0]
-        bias = tiles("bias", 1, [P, A, 8], F32)[0]
+        b_row = tiles("b_row", 1, [P, A, 128], F32)[0]
+        b_dealt = tiles("b_dealt", 1, [P, A, 128], F32)[0]
+        b_turned = tiles("b_turned", 1, [P, A, 128], F32)[0]
         x_all = tiles("x_all", 1, [P, G, 4, 512], F32)[0]
         x_raw = [x_all[:, g] for g in range(G)]
         d_raw = tiles("d_raw", G, [P, 4, 512], F32)
@@ -51,6 +54,9 @@ def tile_mix_lowrank_fm_pl_bias_kernel(tc, x, w4_words, w4_scales, down, up, b, 
         y_q_all = tiles("y_q", 1, [P, A, 512], U32)[0]
         y_q = [y_q_all[:, a] for a in range(A)]
         y_s = tiles("y_s", 1, [P, A, 512], U8)[0]
+
+        def bias(a, r):
+            return b_turned[:, a, 32 * r + BIAS_ROW:32 * r + BIAS_ROW + 1]
 
         def bank(i):
             return psum.tile([P, 512], F32, name="bank%d" % i, tag="bank%d" % i)
@@ -113,30 +119,31 @@ def tile_mix_lowrank_fm_pl_bias_kernel(tc, x, w4_words, w4_scales, down, up, b, 
             nc.sync.dma_start(out=w_raw[a][:].bitcast(I32),
                               in_=w4_words[:, :, 1024 * a:1024 * (a + 1)].rearrange("g p c -> p g c").bitcast(I32))
 
-        def load_scales(queue, a0, a1):
-            for r in range(4):
-                queue.dma_start(out=s_raw[r:P:32, :, 512 * a0:512 * a1].bitcast(I32),
-                                in_=w4_scales[:, r:16:4, 512 * a0:512 * a1].rearrange("g q n -> q g n").bitcast(I32))
+        def load_scales(r, g0, g1):
+            nc.sync.dma_start(out=s_raw[r:P:32, g0:g1].bitcast(I32),
+                              in_=w4_scales[g0:g1, r:16:4].rearrange("g q n -> q g n").bitcast(I32))
 
         def load_rows(dst, rows):
             nc.sync.dma_start(out=dst[:], in_=rows.rearrange("(p j) c -> p j c", j=4))
 
-        def narrow_group(acc, a, r, c0):
+        def narrow_base(acc, a, r, c0):
             cols, ts = slice(128 * a, 128 * (a + 1)), slice(c0, c0 + 128)
             for g in range(G):
                 nc.tensor.matmul_mx(out=acc[:, 0:128], lhsT=w_tile(a, r, g),
                                     lhsT_scale=s_dealt[:, r, g, cols],
                                     rhs=xq[g][1][:, ts].bitcast(FP8X4), rhs_scale=xq[g][2][:, ts], start=(g == 0), stop=False)
-            cols = slice(128 * r, 128 * (r + 1))
+
+        def narrow_branch(acc, a, r, c0):
+            cols, ts = slice(128 * r, 128 * (r + 1)), slice(c0, c0 + 128)
             nc.tensor.matmul_mx(out=acc[:, 0:128], lhsT=uq[a][1][:, cols].bitcast(FP8X4), lhsT_scale=uq[a][2][:, cols],
                                 rhs=hq[1][:, ts].bitcast(FP8X4), rhs_scale=hq[2][:, ts], start=False, stop=True)
-            nc.scalar.activation(out=y_f32[a][:, r, ts], in_=acc[:, 0:128], func=IDENT, bias=bias[:, a, r:r + 1])
+            nc.scalar.activation(out=y_f32[a][:, r, ts], in_=acc[:, 0:128], func=IDENT, bias=bias(a, r))
 
         def drain_v(acc, a, r):
-            nc.vector.tensor_scalar(out=y_f32[a][:, r, :], in0=acc[:], scalar1=bias[:, a, r:r + 1], scalar2=None, op0=ADD)
+            nc.vector.tensor_scalar(out=y_f32[a][:, r, :], in0=acc[:], scalar1=bias(a, r), scalar2=None, op0=ADD)
 
         def drain(acc, a, r):
-            nc.scalar.activation(out=y_f32[a][:, r, :], in_=acc[:], func=IDENT, bias=bias[:, a, r:r + 1])
+            nc.scalar.activation(out=y_f32[a][:, r, :], in_=acc[:], func=IDENT, bias=bias(a, r))
 
         def store_rows(a, r0, r1):
             rows = out_0[512 * a:512 * (a + 1), :].rearrange("(p r) t -> p r t", r=4)
@@ -156,15 +163,17 @@ def tile_mix_lowrank_fm_pl_bias_kernel(tc, x, w4_words, w4_scales, down, up, b, 
                             in_=y_s[OUT_ROW + r:P:32, a0:a1, :].bitcast(I32))
 
         nc.vector.memset(s_raw[:].rearrange("p g n -> p (g n)").bitcast(I32), 0)
+        nc.vector.memset(b_row[:].rearrange("p a c -> p (a c)"), 0.0)
         load_words(0)
-        load_scales(nc.sync, 0, 3)
+        for r in range(4):
+            load_scales(r, 0, 3)
+        nc.sync.dma_start(out=b_row[BIAS_ROW:P:32], in_=b.rearrange("(a q c) -> q a c", a=A, q=4))
         nc.sync.dma_start(out=x_all[:, 0:2], in_=x[0:1024, :].rearrange("(g p j) c -> p g j c", g=2, j=4))
         load_rows(x_raw[2], x[1024:1536, :])
         for g in range(G):
             load_rows(d_raw[g], down[512 * g:512 * (g + 1), :])
         load_words(1)
         load_rows(u_raw[0], up[:, 0:512])
-        nc.sync.dma_start(out=bias[:, :, 0:4], in_=b.rearrange("(a p r) -> p a r", a=A, r=4))
         load_rows(u_raw[1], up[:, 512:1024])
         load_words(2)
         load_rows(u_raw[2], up[:, 1024:1536])
@@ -175,9 +184,13 @@ def tile_mix_lowrank_fm_pl_bias_kernel(tc, x, w4_words, w4_scales, down, up, b, 
         for g in range(G):
             deal_words(0, g)
         deal_scales(0, 3)
+        nc.vector.tensor_copy(out=b_dealt[:].rearrange("p a (r m) -> p a r m", r=4), in_=b_row[:].rearrange("p a (m r) -> p a r m", r=4))
+        for a in range(A):
+            nc.vector.transpose(out=b_turned[:, a], in_=b_dealt[:, a])
         for g in range(G):
-            interleave("s", x_raw[g], xq[g][0], 64, 128)
-            interleave("v", x_raw[g], xq[g][0], 0, 64)
+            cut = 64 if g else 88
+            interleave("s", x_raw[g], xq[g][0], cut, 128)
+            interleave("v", x_raw[g], xq[g][0], 0, cut)
             if g:
                 quantize(xq[g - 1])
         quantize(xq[G - 1])
@@ -185,16 +198,17 @@ def tile_mix_lowrank_fm_pl_bias_kernel(tc, x, w4_words, w4_scales, down, up, b, 
             for r in range(4):
                 base(y0[r], 0, r, g)
         for g in range(G):
-            interleave_dealt("s", d_raw[g], dq[g][0], 2, 4, 0, 80)
-            interleave_dealt("v", d_raw[g], dq[g][0], 0, 2)
-            interleave_dealt("v", d_raw[g], dq[g][0], 2, 4, 80, 128)
+            interleave_dealt("s", d_raw[g], dq[g][0], 0, 2, 88, 128)
+            interleave_dealt("v", d_raw[g], dq[g][0], 0, 2, 0, 88)
+            interleave_dealt("s", d_raw[g], dq[g][0], 2, 4, 0, 44)
+            interleave_dealt("v", d_raw[g], dq[g][0], 2, 4, 44, 128)
             for j in range(4):
                 quantize(dq[g], 128 * j, 128 * (j + 1))
-            for j in range(2):
-                for c in range(4):
+            for j in range(4):
+                for c in range(2):
                     h_pass(g, j, c)
-            for c in range(4):
-                for j in range(2, 4):
+            for c in range(2, 4):
+                for j in range(4):
                     h_pass(g, j, c)
         for g in range(G):
             deal_words(1, g)
@@ -203,69 +217,81 @@ def tile_mix_lowrank_fm_pl_bias_kernel(tc, x, w4_words, w4_scales, down, up, b, 
         h_out("s", 2)
         h_out("s", 3)
         y1 = [bank(4 + r) for r in range(4)]
+        quantize(hq, 0, 128)
         interleave_dealt("v", u_raw[0], uq[0][0], 0, 2)
-        quantize(hq, 0, 256)
-        interleave_dealt("s", u_raw[0], uq[0][0], 2, 4, 0, 48)
-        interleave_dealt("v", u_raw[0], uq[0][0], 2, 4, 48, 128)
+        quantize(hq, 128, 384)
         quantize(uq[0], 0, 256)
-        quantize(hq, 256, 512)
+        quantize(hq, 384, 512)
+        interleave_dealt("s", u_raw[0], uq[0][0], 2, 4, 0, 96)
+        interleave_dealt("v", u_raw[0], uq[0][0], 2, 4, 96, 128)
         quantize(uq[0], 256, 512)
+        interleave_dealt("v", u_raw[1], uq[1][0], 0, 2)
+        interleave_dealt("v", u_raw[1], uq[1][0], 2, 4, 0, 64)
         for r in range(2):
             for g in range(G):
                 base(y1[r], 1, r, g)
-        interleave_dealt("v", u_raw[1], uq[1][0], 0, 2)
-        interleave_dealt("v", u_raw[1], uq[1][0], 2, 4)
+        base(y1[2], 1, 2, 0)
         for r in range(4):
             branch(y0[r], 0, r)
             drain(y0[r], 0, r)
             if r % 2:
                 store_rows(0, r - 1, r + 1)
         quantize(uq[1], 0, 256)
+        interleave_dealt("v", u_raw[1], uq[1][0], 2, 4, 64, 128)
         deal_words(2, 0)
         quantize(uq[1], 256, 512)
         deal_words(2, 1)
         deal_words(2, 2)
-        for r in range(2, 4):
-            for g in range(G):
-                base(y1[r], 1, r, g)
+        for g in range(1, G):
+            base(y1[2], 1, 2, g)
+        base(y1[3], 1, 3, 0)
         for r in range(4):
+            if r == 2:
+                for g in range(1, G):
+                    base(y1[3], 1, 3, g)
             branch(y1[r], 1, r)
             drain(y1[r], 1, r)
             if r % 2:
                 store_rows(1, r - 1, r + 1)
         y2 = [bank(r) for r in range(3)]
-        interleave("v", y_f32[0], y_bf[0], 0, 64)
+        interleave("v", y_f32[0], y_bf[0], 0, 48)
         interleave_dealt("v", u_raw[2], uq[2][0], 0, 2)
-        interleave("v", y_f32[0], y_bf[0], 64, 128)
+        interleave("v", y_f32[0], y_bf[0], 48, 80)
         quantize(uq[2], 0, 256)
+        interleave("v", y_f32[0], y_bf[0], 80, 128)
+        interleave_dealt("s", u_raw[2], uq[2][0], 2, 4, 0, 64)
+        interleave_dealt("v", u_raw[2], uq[2][0], 2, 4, 64, 128)
         quantize_y(0)
-        interleave_dealt("v", u_raw[2], uq[2][0], 2, 4)
         store_words(0)
-        interleave("v", y_f32[1], y_bf[1], 0, 32)
         quantize(uq[2], 256, 512)
-        interleave("v", y_f32[1], y_bf[1], 32, 96)
+        interleave("s", y_f32[1], y_bf[1], 112, 128)
+        interleave("v", y_f32[1], y_bf[1], 0, 64)
+        interleave("v", y_f32[1], y_bf[1], 64, 96)
         for r in range(2):
             for g in range(G):
                 base(y2[r], 2, r, g)
-        interleave("s", y_f32[1], y_bf[1], 96, 128)
         for r in range(2):
             branch(y2[r], 2, r)
             drain(y2[r], 2, r)
         store_rows(2, 0, 2)
-        quantize_y(1)
+        interleave("s", y_f32[1], y_bf[1], 96, 112)
+        quantize_y(1, 0, 256)
+        quantize_y(1, 256, 512)
         store_words(1)
         for g in range(G):
             base(y2[2], 2, 2, g)
         branch(y2[2], 2, 2)
         drain(y2[2], 2, 2)
         for c in range(4):
-            narrow_group(bank(4 + c), 2, 3, 128 * c)
+            acc = bank(4 + c)
+            narrow_base(acc, 2, 3, 128 * c)
+            narrow_branch(acc, 2, 3, 128 * c)
         store_rows(2, 2, 4)
         interleave("v", y_f32[2], y_bf[2], 0, 32)
         interleave("v", y_f32[2], y_bf[2], 32, 64)
         quantize_y(2, 0, 128)
-        interleave("s", y_f32[2], y_bf[2], 104, 128)
-        interleave("v", y_f32[2], y_bf[2], 64, 104)
+        interleave("s", y_f32[2], y_bf[2], 96, 128)
+        interleave("v", y_f32[2], y_bf[2], 64, 96)
         quantize_y(2, 128, 256)
         quantize_y(2, 256, 384)
         quantize_y(2, 384, 512)

@@ -42,7 +42,8 @@ def tile_mix_lowrank_fm_pl_bias_kernel(tc, x, w4_words, w4_scales, down, up, b, 
         b_turned = tiles("b_turned", 1, [P, A, 128], F32)[0]
         x_all = tiles("x_all", 1, [P, G, 4, 512], F32)[0]
         x_raw = [x_all[:, g] for g in range(G)]
-        d_raw = tiles("d_raw", G, [P, 4, 512], F32)
+        d_raw = tiles("d_raw", G - 1, [P, 4, 512], F32)
+        d_last = tiles("d_last", 2, [P, 4, 256], F32)
         u_raw = tiles("u_raw", A, [P, 4, 512], F32)
         y_f32 = tiles("y_f32", A, [P, 4, 512], F32)
 
@@ -76,6 +77,11 @@ def tile_mix_lowrank_fm_pl_bias_kernel(tc, x, w4_words, w4_scales, down, up, b, 
             copy(engine,
                  dst[:, 512 * i0:512 * i1].rearrange("p (i m j) -> p m j i", m=128, j=4)[:, m0:m1],
                  src[:].rearrange("p j (m i) -> p m j i", i=4)[:, m0:m1, :, i0:i1])
+
+        def interleave_half(engine, half, i0, i1, m0=0, m1=64):
+            copy(engine,
+                 dq[2][0][:, 512 * i0:512 * i1].rearrange("p (i m j) -> p m j i", m=128, j=4)[:, 64 * half + m0:64 * half + m1],
+                 d_last[half][:].rearrange("p j (m i) -> p m j i", i=4)[:, m0:m1, :, i0:i1])
 
         def h_pass(g, j, c):
             cols, ts = slice(128 * j, 128 * (j + 1)), slice(128 * c, 128 * (c + 1))
@@ -133,11 +139,14 @@ def tile_mix_lowrank_fm_pl_bias_kernel(tc, x, w4_words, w4_scales, down, up, b, 
                                     lhsT_scale=s_dealt[:, r, g, cols],
                                     rhs=xq[g][1][:, ts].bitcast(FP8X4), rhs_scale=xq[g][2][:, ts], start=(g == 0), stop=False)
 
-        def narrow_branch(acc, a, r, c0):
+        def narrow_branch(acc, a, r, c0, engine):
             cols, ts = slice(128 * r, 128 * (r + 1)), slice(c0, c0 + 128)
             nc.tensor.matmul_mx(out=acc[:, 0:128], lhsT=uq[a][1][:, cols].bitcast(FP8X4), lhsT_scale=uq[a][2][:, cols],
                                 rhs=hq[1][:, ts].bitcast(FP8X4), rhs_scale=hq[2][:, ts], start=False, stop=True)
-            nc.scalar.activation(out=y_f32[a][:, r, ts], in_=acc[:, 0:128], func=IDENT, bias=bias(a, r))
+            if engine == "v":
+                nc.vector.tensor_scalar(out=y_f32[a][:, r, ts], in0=acc[:, 0:128], scalar1=bias(a, r), scalar2=None, op0=ADD)
+            else:
+                nc.scalar.activation(out=y_f32[a][:, r, ts], in_=acc[:, 0:128], func=IDENT, bias=bias(a, r))
 
         def drain_v(acc, a, r):
             nc.vector.tensor_scalar(out=y_f32[a][:, r, :], in0=acc[:], scalar1=bias(a, r), scalar2=None, op0=ADD)
@@ -167,12 +176,14 @@ def tile_mix_lowrank_fm_pl_bias_kernel(tc, x, w4_words, w4_scales, down, up, b, 
         load_words(0)
         for r in range(4):
             load_scales(r, 0, 3)
-        nc.sync.dma_start(out=b_row[BIAS_ROW:P:32], in_=b.rearrange("(a q c) -> q a c", a=A, q=4))
         nc.sync.dma_start(out=x_all[:, 0:2], in_=x[0:1024, :].rearrange("(g p j) c -> p g j c", g=2, j=4))
         load_rows(x_raw[2], x[1024:1536, :])
-        for g in range(G):
+        for g in range(G - 1):
             load_rows(d_raw[g], down[512 * g:512 * (g + 1), :])
+        for half in range(2):
+            load_rows(d_last[half], down[1024:1536, 256 * half:256 * (half + 1)])
         load_words(1)
+        nc.sync.dma_start(out=b_row[BIAS_ROW:P:32], in_=b.rearrange("(a q c) -> q a c", a=A, q=4))
         load_rows(u_raw[0], up[:, 0:512])
         load_rows(u_raw[1], up[:, 512:1024])
         load_words(2)
@@ -184,9 +195,6 @@ def tile_mix_lowrank_fm_pl_bias_kernel(tc, x, w4_words, w4_scales, down, up, b, 
         for g in range(G):
             deal_words(0, g)
         deal_scales(0, 3)
-        nc.vector.tensor_copy(out=b_dealt[:].rearrange("p a (r m) -> p a r m", r=4), in_=b_row[:].rearrange("p a (m r) -> p a r m", r=4))
-        for a in range(A):
-            nc.vector.transpose(out=b_turned[:, a], in_=b_dealt[:, a])
         for g in range(G):
             cut = 64 if g else 88
             interleave("s", x_raw[g], xq[g][0], cut, 128)
@@ -194,22 +202,32 @@ def tile_mix_lowrank_fm_pl_bias_kernel(tc, x, w4_words, w4_scales, down, up, b, 
             if g:
                 quantize(xq[g - 1])
         quantize(xq[G - 1])
-        for g in range(G):
+        for g in range(G - 1):
             for r in range(4):
                 base(y0[r], 0, r, g)
-        for g in range(G):
+        for g in range(G - 1):
             interleave_dealt("s", d_raw[g], dq[g][0], 0, 2, 88, 128)
             interleave_dealt("v", d_raw[g], dq[g][0], 0, 2, 0, 88)
             interleave_dealt("s", d_raw[g], dq[g][0], 2, 4, 0, 44)
             interleave_dealt("v", d_raw[g], dq[g][0], 2, 4, 44, 128)
-            for j in range(4):
-                quantize(dq[g], 128 * j, 128 * (j + 1))
-            for j in range(4):
-                for c in range(2):
-                    h_pass(g, j, c)
-            for c in range(2, 4):
+            quantize(dq[g], 0, 256)
+            quantize(dq[g], 256, 512)
+            for c in range(4):
                 for j in range(4):
                     h_pass(g, j, c)
+            if g == 0:
+                for r in range(4):
+                    base(y0[r], 0, r, G - 1)
+        for half in range(2):
+            interleave_half("s", half, 2, 4, 0, 44)
+            interleave_half("v", half, 0, 2)
+            interleave_half("v", half, 2, 4, 44, 64)
+            for j in range(4):
+                quantize(dq[2], 128 * j + 64 * half, 128 * j + 64 * (half + 1))
+        for c in range(4):
+            for j in range(4):
+                h_pass(2, j, c)
+        nc.scalar.copy(out=b_dealt[:].rearrange("p a (r m) -> p a r m", r=4), in_=b_row[:].rearrange("p a (m r) -> p a r m", r=4))
         for g in range(G):
             deal_words(1, g)
         h_out("s", 0)
@@ -217,84 +235,89 @@ def tile_mix_lowrank_fm_pl_bias_kernel(tc, x, w4_words, w4_scales, down, up, b, 
         h_out("s", 2)
         h_out("s", 3)
         y1 = [bank(4 + r) for r in range(4)]
-        quantize(hq, 0, 128)
-        interleave_dealt("v", u_raw[0], uq[0][0], 0, 2)
-        quantize(hq, 128, 384)
+        nc.vector.transpose(out=b_turned[:, 0], in_=b_dealt[:, 0])
+        quantize(hq, 0, 256)
+        interleave_dealt("s", u_raw[0], uq[0][0], 0, 2, 88, 128)
+        interleave_dealt("v", u_raw[0], uq[0][0], 0, 2, 0, 88)
+        quantize(hq, 256, 512)
         quantize(uq[0], 0, 256)
-        quantize(hq, 384, 512)
         interleave_dealt("s", u_raw[0], uq[0][0], 2, 4, 0, 96)
         interleave_dealt("v", u_raw[0], uq[0][0], 2, 4, 96, 128)
+        for a in range(1, A):
+            nc.vector.transpose(out=b_turned[:, a], in_=b_dealt[:, a])
         quantize(uq[0], 256, 512)
-        interleave_dealt("v", u_raw[1], uq[1][0], 0, 2)
-        interleave_dealt("v", u_raw[1], uq[1][0], 2, 4, 0, 64)
         for r in range(2):
             for g in range(G):
                 base(y1[r], 1, r, g)
-        base(y1[2], 1, 2, 0)
+        for g in range(G - 1):
+            base(y1[2], 1, 2, g)
         for r in range(4):
+            if r == 2:
+                base(y1[2], 1, 2, G - 1)
             branch(y0[r], 0, r)
             drain(y0[r], 0, r)
             if r % 2:
                 store_rows(0, r - 1, r + 1)
+        interleave_dealt("v", u_raw[1], uq[1][0], 0, 2)
+        interleave_dealt("v", u_raw[1], uq[1][0], 2, 4, 0, 64)
         quantize(uq[1], 0, 256)
         interleave_dealt("v", u_raw[1], uq[1][0], 2, 4, 64, 128)
         deal_words(2, 0)
         quantize(uq[1], 256, 512)
         deal_words(2, 1)
         deal_words(2, 2)
-        for g in range(1, G):
-            base(y1[2], 1, 2, g)
-        base(y1[3], 1, 3, 0)
+        for g in range(G):
+            base(y1[3], 1, 3, g)
+        y2 = [bank(r) for r in range(3)]
         for r in range(4):
             if r == 2:
-                for g in range(1, G):
-                    base(y1[3], 1, 3, g)
+                base(y2[0], 2, 0, 0)
             branch(y1[r], 1, r)
             drain(y1[r], 1, r)
             if r % 2:
                 store_rows(1, r - 1, r + 1)
-        y2 = [bank(r) for r in range(3)]
-        interleave("v", y_f32[0], y_bf[0], 0, 48)
+        interleave("v", y_f32[0], y_bf[0], 0, 32)
         interleave_dealt("v", u_raw[2], uq[2][0], 0, 2)
-        interleave("v", y_f32[0], y_bf[0], 48, 80)
-        quantize(uq[2], 0, 256)
-        interleave("v", y_f32[0], y_bf[0], 80, 128)
-        interleave_dealt("s", u_raw[2], uq[2][0], 2, 4, 0, 64)
-        interleave_dealt("v", u_raw[2], uq[2][0], 2, 4, 64, 128)
+        interleave("v", y_f32[0], y_bf[0], 32, 64)
+        quantize(uq[2], 0, 128)
+        quantize(uq[2], 128, 256)
+        interleave("v", y_f32[0], y_bf[0], 64, 128)
+        interleave_dealt("s", u_raw[2], uq[2][0], 2, 4, 0, 72)
+        interleave_dealt("v", u_raw[2], uq[2][0], 2, 4, 72, 128)
         quantize_y(0)
         store_words(0)
         quantize(uq[2], 256, 512)
-        interleave("s", y_f32[1], y_bf[1], 112, 128)
-        interleave("v", y_f32[1], y_bf[1], 0, 64)
-        interleave("v", y_f32[1], y_bf[1], 64, 96)
         for r in range(2):
-            for g in range(G):
+            for g in range(1 - r, G):
                 base(y2[r], 2, r, g)
         for r in range(2):
             branch(y2[r], 2, r)
             drain(y2[r], 2, r)
         store_rows(2, 0, 2)
-        interleave("s", y_f32[1], y_bf[1], 96, 112)
+        interleave("v", y_f32[1], y_bf[1], 0, 64)
+        interleave("v", y_f32[1], y_bf[1], 64, 96)
+        interleave("s", y_f32[1], y_bf[1], 96, 128)
         quantize_y(1, 0, 256)
         quantize_y(1, 256, 512)
         store_words(1)
         for g in range(G):
             base(y2[2], 2, 2, g)
+        last = [bank(4 + c) for c in range(4)]
+        for c in range(2):
+            narrow_base(last[c], 2, 3, 128 * c)
         branch(y2[2], 2, 2)
         drain(y2[2], 2, 2)
         for c in range(4):
-            acc = bank(4 + c)
-            narrow_base(acc, 2, 3, 128 * c)
-            narrow_branch(acc, 2, 3, 128 * c)
+            if c >= 2:
+                narrow_base(last[c], 2, 3, 128 * c)
+            narrow_branch(last[c], 2, 3, 128 * c, "v" if c < 2 else "s")
         store_rows(2, 2, 4)
         interleave("v", y_f32[2], y_bf[2], 0, 32)
         interleave("v", y_f32[2], y_bf[2], 32, 64)
-        quantize_y(2, 0, 128)
-        interleave("s", y_f32[2], y_bf[2], 96, 128)
-        interleave("v", y_f32[2], y_bf[2], 64, 96)
-        quantize_y(2, 128, 256)
-        quantize_y(2, 256, 384)
-        quantize_y(2, 384, 512)
+        interleave("s", y_f32[2], y_bf[2], 64, 96)
+        interleave("v", y_f32[2], y_bf[2], 96, 128)
+        quantize_y(2, 0, 256)
+        quantize_y(2, 256, 512)
         store_words(2)
         for q in range(4):
             store_scales(nc.scalar if q % 2 else nc.sync, 0, 3, q)

@@ -34,7 +34,7 @@ def tile_mix_lowrank_fm_pl_bias_kernel(tc, x, w4_words, w4_scales, down, up, b, 
             return [sb.tile(shape, dtype, name="%s%d" % (name, i), align_bytes=256) for i in range(n)]
 
         w_raw = tiles("w_raw", A, [P, G, 1024], U8)
-        w_dealt = [tiles("w_dealt%d_" % a, G, [P, 4, 256], U8) for a in range(A)]
+        w_dealt = tiles("w_dealt", A, [P, G, 4, 256], U8)
         s_raw = tiles("s_raw", 1, [P, G, M], U8)[0]
         s_dealt = tiles("s_dealt", 1, [P, 4, G, M // 4], U8)[0]
         b_row = tiles("b_row", 1, [P, A, 128], F32)[0]
@@ -42,8 +42,7 @@ def tile_mix_lowrank_fm_pl_bias_kernel(tc, x, w4_words, w4_scales, down, up, b, 
         b_turned = tiles("b_turned", 1, [P, A, 128], F32)[0]
         x_all = tiles("x_all", 1, [P, G, 4, 512], F32)[0]
         x_raw = [x_all[:, g] for g in range(G)]
-        d_raw = tiles("d_raw", G - 1, [P, 4, 512], F32)
-        d_last = tiles("d_last", 2, [P, 4, 256], F32)
+        d_raw = tiles("d_raw", G, [P, 4, 512], F32)
         u_raw = tiles("u_raw", A, [P, 4, 512], F32)
         y_f32 = tiles("y_f32", A, [P, 4, 512], F32)
 
@@ -78,11 +77,6 @@ def tile_mix_lowrank_fm_pl_bias_kernel(tc, x, w4_words, w4_scales, down, up, b, 
                  dst[:, 512 * i0:512 * i1].rearrange("p (i m j) -> p m j i", m=128, j=4)[:, m0:m1],
                  src[:].rearrange("p j (m i) -> p m j i", i=4)[:, m0:m1, :, i0:i1])
 
-        def interleave_half(engine, half, i0, i1, m0=0, m1=64):
-            copy(engine,
-                 dq[2][0][:, 512 * i0:512 * i1].rearrange("p (i m j) -> p m j i", m=128, j=4)[:, 64 * half + m0:64 * half + m1],
-                 d_last[half][:].rearrange("p j (m i) -> p m j i", i=4)[:, m0:m1, :, i0:i1])
-
         def h_pass(g, j, c):
             cols, ts = slice(128 * j, 128 * (j + 1)), slice(128 * c, 128 * (c + 1))
             nc.tensor.matmul_mx(out=hb[c][:, cols], lhsT=dq[g][1][:, cols].bitcast(FP8X4), lhsT_scale=dq[g][2][:, cols],
@@ -110,12 +104,12 @@ def tile_mix_lowrank_fm_pl_bias_kernel(tc, x, w4_words, w4_scales, down, up, b, 
         def branch(acc, a, r):
             mm8(acc, uq[a], r, hq, False, True)
 
-        def deal_words(a, g):
-            nc.vector.tensor_copy(out=w_dealt[a][g][:].bitcast(U16),
-                                  in_=w_raw[a][:, g].bitcast(U16).rearrange("p (m r) -> p r m", r=4))
+        def deal_words(a, g0, g1):
+            nc.vector.tensor_copy(out=w_dealt[a][:, g0:g1].bitcast(U16),
+                                  in_=w_raw[a][:, g0:g1].bitcast(U16).rearrange("p g (m r) -> p g r m", r=4))
 
         def w_tile(a, r, g):
-            return w_dealt[a][g][:, r].bitcast(FP4X4)
+            return w_dealt[a][:, g, r].bitcast(FP4X4)
 
         def deal_scales(a0, a1):
             nc.vector.tensor_copy(out=s_dealt[:, :, :, 128 * a0:128 * a1],
@@ -176,14 +170,12 @@ def tile_mix_lowrank_fm_pl_bias_kernel(tc, x, w4_words, w4_scales, down, up, b, 
         load_words(0)
         for r in range(4):
             load_scales(r, 0, 3)
+        nc.sync.dma_start(out=b_row[BIAS_ROW:P:32], in_=b.rearrange("(a q c) -> q a c", a=A, q=4))
         nc.sync.dma_start(out=x_all[:, 0:2], in_=x[0:1024, :].rearrange("(g p j) c -> p g j c", g=2, j=4))
         load_rows(x_raw[2], x[1024:1536, :])
-        for g in range(G - 1):
+        for g in range(G):
             load_rows(d_raw[g], down[512 * g:512 * (g + 1), :])
-        for half in range(2):
-            load_rows(d_last[half], down[1024:1536, 256 * half:256 * (half + 1)])
         load_words(1)
-        nc.sync.dma_start(out=b_row[BIAS_ROW:P:32], in_=b.rearrange("(a q c) -> q a c", a=A, q=4))
         load_rows(u_raw[0], up[:, 0:512])
         load_rows(u_raw[1], up[:, 512:1024])
         load_words(2)
@@ -192,9 +184,12 @@ def tile_mix_lowrank_fm_pl_bias_kernel(tc, x, w4_words, w4_scales, down, up, b, 
         y0 = [bank(r) for r in range(4)]
         hb = [bank(4 + c) for c in range(4)]
 
-        for g in range(G):
-            deal_words(0, g)
+        deal_words(0, 0, 2)
+        deal_words(0, 2, 3)
         deal_scales(0, 3)
+        nc.vector.tensor_copy(out=b_dealt[:].rearrange("p a (r m) -> p a r m", r=4), in_=b_row[:].rearrange("p a (m r) -> p a r m", r=4))
+        for a in range(A):
+            nc.vector.transpose(out=b_turned[:, a], in_=b_dealt[:, a])
         for g in range(G):
             cut = 64 if g else 88
             interleave("s", x_raw[g], xq[g][0], cut, 128)
@@ -218,99 +213,100 @@ def tile_mix_lowrank_fm_pl_bias_kernel(tc, x, w4_words, w4_scales, down, up, b, 
             if g == 0:
                 for r in range(4):
                     base(y0[r], 0, r, G - 1)
-        for half in range(2):
-            interleave_half("s", half, 2, 4, 0, 44)
-            interleave_half("v", half, 0, 2)
-            interleave_half("v", half, 2, 4, 44, 64)
-            for j in range(4):
-                quantize(dq[2], 128 * j + 64 * half, 128 * j + 64 * (half + 1))
-        for c in range(4):
+        interleave_dealt("s", d_raw[2], dq[2][0], 0, 2, 88, 128)
+        interleave_dealt("v", d_raw[2], dq[2][0], 0, 2, 0, 88)
+        interleave_dealt("s", d_raw[2], dq[2][0], 2, 4, 0, 44)
+        interleave_dealt("v", d_raw[2], dq[2][0], 2, 4, 44, 128)
+        for j in range(4):
+            quantize(dq[2], 128 * j, 128 * (j + 1))
+        for j in range(4):
+            for c in range(2):
+                h_pass(2, j, c)
+        for c in range(2, 4):
             for j in range(4):
                 h_pass(2, j, c)
-        nc.scalar.copy(out=b_dealt[:].rearrange("p a (r m) -> p a r m", r=4), in_=b_row[:].rearrange("p a (m r) -> p a r m", r=4))
-        for g in range(G):
-            deal_words(1, g)
+        deal_words(1, 0, 2)
+        deal_words(1, 2, 3)
         h_out("s", 0)
         h_out("v", 1)
         h_out("s", 2)
         h_out("s", 3)
         y1 = [bank(4 + r) for r in range(4)]
-        nc.vector.transpose(out=b_turned[:, 0], in_=b_dealt[:, 0])
         quantize(hq, 0, 256)
-        interleave_dealt("s", u_raw[0], uq[0][0], 0, 2, 88, 128)
-        interleave_dealt("v", u_raw[0], uq[0][0], 0, 2, 0, 88)
+        interleave_dealt("s", u_raw[0], uq[0][0], 0, 2, 104, 128)
+        interleave_dealt("v", u_raw[0], uq[0][0], 0, 2, 0, 104)
         quantize(hq, 256, 512)
-        quantize(uq[0], 0, 256)
+        quantize(uq[0], 0, 128)
+        quantize(uq[0], 128, 256)
         interleave_dealt("s", u_raw[0], uq[0][0], 2, 4, 0, 96)
         interleave_dealt("v", u_raw[0], uq[0][0], 2, 4, 96, 128)
-        for a in range(1, A):
-            nc.vector.transpose(out=b_turned[:, a], in_=b_dealt[:, a])
         quantize(uq[0], 256, 512)
         for r in range(2):
             for g in range(G):
                 base(y1[r], 1, r, g)
-        for g in range(G - 1):
-            base(y1[2], 1, 2, g)
+        base(y1[2], 1, 2, 0)
         for r in range(4):
             if r == 2:
-                base(y1[2], 1, 2, G - 1)
+                base(y1[2], 1, 2, 1)
             branch(y0[r], 0, r)
             drain(y0[r], 0, r)
             if r % 2:
                 store_rows(0, r - 1, r + 1)
         interleave_dealt("v", u_raw[1], uq[1][0], 0, 2)
         interleave_dealt("v", u_raw[1], uq[1][0], 2, 4, 0, 64)
-        quantize(uq[1], 0, 256)
+        quantize(uq[1], 0, 128)
+        quantize(uq[1], 128, 256)
         interleave_dealt("v", u_raw[1], uq[1][0], 2, 4, 64, 128)
-        deal_words(2, 0)
+        deal_words(2, 0, 1)
         quantize(uq[1], 256, 512)
-        deal_words(2, 1)
-        deal_words(2, 2)
-        for g in range(G):
+        deal_words(2, 1, 3)
+        base(y1[2], 1, 2, 2)
+        for g in range(G - 1):
             base(y1[3], 1, 3, g)
         y2 = [bank(r) for r in range(3)]
         for r in range(4):
             if r == 2:
+                base(y1[3], 1, 3, G - 1)
                 base(y2[0], 2, 0, 0)
             branch(y1[r], 1, r)
             drain(y1[r], 1, r)
             if r % 2:
                 store_rows(1, r - 1, r + 1)
-        interleave("v", y_f32[0], y_bf[0], 0, 32)
+        interleave("v", y_f32[0], y_bf[0], 0, 64)
         interleave_dealt("v", u_raw[2], uq[2][0], 0, 2)
-        interleave("v", y_f32[0], y_bf[0], 32, 64)
+        quantize_y(0, 0, 256)
         quantize(uq[2], 0, 128)
         quantize(uq[2], 128, 256)
+        interleave_dealt("s", u_raw[2], uq[2][0], 2, 4, 0, 88)
+        interleave_dealt("v", u_raw[2], uq[2][0], 2, 4, 88, 128)
+        interleave("s", y_f32[1], y_bf[1], 112, 128)
         interleave("v", y_f32[0], y_bf[0], 64, 128)
-        interleave_dealt("s", u_raw[2], uq[2][0], 2, 4, 0, 72)
-        interleave_dealt("v", u_raw[2], uq[2][0], 2, 4, 72, 128)
-        quantize_y(0)
-        store_words(0)
         quantize(uq[2], 256, 512)
+        quantize_y(0, 256, 512)
+        store_words(0)
         for r in range(2):
             for g in range(1 - r, G):
                 base(y2[r], 2, r, g)
+        base(y2[2], 2, 2, 0)
         for r in range(2):
             branch(y2[r], 2, r)
             drain(y2[r], 2, r)
         store_rows(2, 0, 2)
+        for g in range(1, G):
+            base(y2[2], 2, 2, g)
         interleave("v", y_f32[1], y_bf[1], 0, 64)
-        interleave("v", y_f32[1], y_bf[1], 64, 96)
-        interleave("s", y_f32[1], y_bf[1], 96, 128)
+        interleave("v", y_f32[1], y_bf[1], 64, 112)
         quantize_y(1, 0, 256)
         quantize_y(1, 256, 512)
         store_words(1)
-        for g in range(G):
-            base(y2[2], 2, 2, g)
         last = [bank(4 + c) for c in range(4)]
-        for c in range(2):
-            narrow_base(last[c], 2, 3, 128 * c)
+        narrow_base(last[0], 2, 3, 0)
         branch(y2[2], 2, 2)
         drain(y2[2], 2, 2)
         for c in range(4):
-            if c >= 2:
+            if c:
                 narrow_base(last[c], 2, 3, 128 * c)
-            narrow_branch(last[c], 2, 3, 128 * c, "v" if c < 2 else "s")
+            narrow_branch(last[c], 2, 3, 128 * c, "s")
         store_rows(2, 2, 4)
         interleave("v", y_f32[2], y_bf[2], 0, 32)
         interleave("v", y_f32[2], y_bf[2], 32, 64)

@@ -314,6 +314,6 @@ def tile_mix_lowrank_fm_pl_bias_kernel(tc, x, w4_words, w4_scales, down, up, b, 
         interleave("v", y_f32[2], y_bf[2], 96, 128)
         quantize_y(2, 0, 256)
         quantize_y(2, 256, 512)
-        store_words(2)
         for q in range(4):
             store_scales(nc.scalar if q % 2 else nc.sync, 0, 3, q)
+        store_words(2)

@@ -67,7 +67,7 @@ def tile_mix_lowrank_fm_pl_bias_kernel(tc, x, w4_words, w4_scales, down, up, b, 
             else:
                 nc.scalar.copy(out=out, in_=in_)
 
-        def interleave(engine, src, dst, m0, m1, run=2):
+        def interleave(engine, src, dst, m0, m1, run=4):
             copy(engine,
                  dst[:, 16 * m0:16 * m1].rearrange("p (m i j) -> p m j i", i=run, j=4),
                  src[:, :, 4 * m0:4 * m1].rearrange("p j (m i) -> p m j i", i=run))

@@ -40,8 +40,9 @@ def tile_mix_lowrank_fm_pl_bias_kernel(tc, x, w4_words, w4_scales, down, up, b, 
         b_row = tiles("b_row", 1, [P, A, 128], F32)[0]
         b_dealt = tiles("b_dealt", 1, [P, A, 128], F32)[0]
         b_turned = tiles("b_turned", 1, [P, A, 128], F32)[0]
-        x_all = tiles("x_all", 1, [P, G, 4, 512], F32)[0]
-        x_raw = [x_all[:, g] for g in range(G)]
+        x_all = tiles("x_all", 1, [P, 2, 4, 512], F32)[0]
+        x_raw = [x_all[:, g] for g in range(2)]
+        x_last = tiles("x_last", 2, [P, 4, 256], F32)
         d_raw = tiles("d_raw", G, [P, 4, 512], F32)
         u_raw = tiles("u_raw", A, [P, 4, 512], F32)
         y_f32 = tiles("y_f32", A, [P, 4, 512], F32)
@@ -165,16 +166,25 @@ def tile_mix_lowrank_fm_pl_bias_kernel(tc, x, w4_words, w4_scales, down, up, b, 
             queue.dma_start(out=out_2[a0:a1, r:16:4, :].rearrange("a q t -> q a t").bitcast(I32),
                             in_=y_s[OUT_ROW + r:P:32, a0:a1, :].bitcast(I32))
 
+        def round_last(engine, h, m0, m1):
+            interleave(engine, x_last[h], xq[2][0][:, 1024 * h:1024 * (h + 1)], m0, m1)
+
+        def half_base(acc, r, h):
+            ts = slice(256 * h, 256 * (h + 1))
+            nc.tensor.matmul_mx(out=acc[:, ts], lhsT=w_tile(0, r, 2), lhsT_scale=s_dealt[:, r, 2, 0:128],
+                                rhs=xq[2][1][:, ts].bitcast(FP8X4), rhs_scale=xq[2][2][:, ts], start=False, stop=False)
+
         nc.vector.memset(s_raw[:].rearrange("p g n -> p (g n)").bitcast(I32), 0)
         nc.vector.memset(b_row[:].rearrange("p a c -> p (a c)"), 0.0)
         load_words(0)
         for r in range(4):
             load_scales(r, 0, 3)
         nc.sync.dma_start(out=b_row[BIAS_ROW:P:32], in_=b.rearrange("(a q c) -> q a c", a=A, q=4))
-        nc.sync.dma_start(out=x_all[:, 0:2], in_=x[0:1024, :].rearrange("(g p j) c -> p g j c", g=2, j=4))
-        load_rows(x_raw[2], x[1024:1536, :])
+        nc.sync.dma_start(out=x_all[:], in_=x[0:1024, :].rearrange("(g p j) c -> p g j c", g=2, j=4))
         for g in range(G):
             load_rows(d_raw[g], down[512 * g:512 * (g + 1), :])
+        for h in range(2):
+            load_rows(x_last[h], x[1024:1536, 256 * h:256 * (h + 1)])
         load_words(1)
         load_rows(u_raw[0], up[:, 0:512])
         load_rows(u_raw[1], up[:, 512:1024])
@@ -190,49 +200,46 @@ def tile_mix_lowrank_fm_pl_bias_kernel(tc, x, w4_words, w4_scales, down, up, b, 
         nc.vector.tensor_copy(out=b_dealt[:].rearrange("p a (r m) -> p a r m", r=4), in_=b_row[:].rearrange("p a (m r) -> p a r m", r=4))
         for a in range(A):
             nc.vector.transpose(out=b_turned[:, a], in_=b_dealt[:, a])
+        interleave("s", x_raw[0], xq[0][0], 88, 128)
+        interleave("v", x_raw[0], xq[0][0], 0, 88)
+        interleave("s", x_raw[1], xq[1][0], 40, 128)
+        interleave("v", x_raw[1], xq[1][0], 0, 40)
+        quantize(xq[0])
+        for r in range(4):
+            base(y0[r], 0, r, 0)
         for g in range(G):
-            cut = 64 if g else 88
-            interleave("s", x_raw[g], xq[g][0], cut, 128)
-            interleave("v", x_raw[g], xq[g][0], 0, cut)
-            if g:
-                quantize(xq[g - 1])
-        quantize(xq[G - 1])
-        for g in range(G - 1):
-            for r in range(4):
-                base(y0[r], 0, r, g)
-        for g in range(G - 1):
             interleave_dealt("s", d_raw[g], dq[g][0], 0, 2, 88, 128)
             interleave_dealt("v", d_raw[g], dq[g][0], 0, 2, 0, 88)
-            interleave_dealt("s", d_raw[g], dq[g][0], 2, 4, 0, 44)
-            interleave_dealt("v", d_raw[g], dq[g][0], 2, 4, 44, 128)
+            interleave_dealt("s", d_raw[g], dq[g][0], 2, 4, 0, 56)
+            interleave_dealt("v", d_raw[g], dq[g][0], 2, 4, 56, 128)
             quantize(dq[g], 0, 256)
             quantize(dq[g], 256, 512)
-            for c in range(4):
-                for j in range(4):
-                    h_pass(g, j, c)
             if g == 0:
-                for r in range(4):
-                    base(y0[r], 0, r, G - 1)
-        interleave_dealt("s", d_raw[2], dq[2][0], 0, 2, 88, 128)
-        interleave_dealt("v", d_raw[2], dq[2][0], 0, 2, 0, 88)
-        interleave_dealt("s", d_raw[2], dq[2][0], 2, 4, 0, 44)
-        interleave_dealt("v", d_raw[2], dq[2][0], 2, 4, 44, 128)
-        for j in range(4):
-            quantize(dq[2], 128 * j, 128 * (j + 1))
-        for j in range(4):
-            for c in range(2):
-                h_pass(2, j, c)
-        for c in range(2, 4):
-            for j in range(4):
-                h_pass(2, j, c)
+                quantize(xq[1])
+            if g < 2:
+                for c in range(4):
+                    for j in range(4):
+                        h_pass(g, j, c)
+        for r in range(4):
+            base(y0[r], 0, r, 1)
+        for h in range(2):
+            round_last("s", h, 40, 64)
+            round_last("v", h, 0, 40)
+            quantize(xq[2], 256 * h, 256 * h + 128)
+            quantize(xq[2], 256 * h + 128, 256 * h + 256)
+            for c in range(2 * h, 2 * h + 2):
+                for j in range(4):
+                    h_pass(2, j, c)
+            for r in range(4):
+                half_base(y0[r], r, h)
+        h_out("s", 0)
+        h_out("s", 1)
         deal_words(1, 0, 2)
         deal_words(1, 2, 3)
-        h_out("s", 0)
-        h_out("v", 1)
         h_out("s", 2)
-        h_out("s", 3)
-        y1 = [bank(4 + r) for r in range(4)]
         quantize(hq, 0, 256)
+        h_out("v", 3)
+        y1 = [bank(4 + r) for r in range(4)]
         interleave_dealt("s", u_raw[0], uq[0][0], 0, 2, 104, 128)
         interleave_dealt("v", u_raw[0], uq[0][0], 0, 2, 0, 104)
         quantize(hq, 256, 512)

@@ -240,8 +240,8 @@ def tile_mix_lowrank_fm_pl_bias_kernel(tc, x, w4_words, w4_scales, down, up, b, 
         quantize(hq, 0, 256)
         h_out("v", 3)
         y1 = [bank(4 + r) for r in range(4)]
-        interleave_dealt("s", u_raw[0], uq[0][0], 0, 2, 104, 128)
-        interleave_dealt("v", u_raw[0], uq[0][0], 0, 2, 0, 104)
+        interleave_dealt("s", u_raw[0], uq[0][0], 0, 2, 88, 128)
+        interleave_dealt("v", u_raw[0], uq[0][0], 0, 2, 0, 88)
         quantize(hq, 256, 512)
         quantize(uq[0], 0, 128)
         quantize(uq[0], 128, 256)
@@ -251,9 +251,9 @@ def tile_mix_lowrank_fm_pl_bias_kernel(tc, x, w4_words, w4_scales, down, up, b, 
         for r in range(2):
             for g in range(G):
                 base(y1[r], 1, r, g)
-        base(y1[2], 1, 2, 0)
         for r in range(4):
             if r == 2:
+                base(y1[2], 1, 2, 0)
                 base(y1[2], 1, 2, 1)
             branch(y0[r], 0, r)
             drain(y0[r], 0, r)
@@ -268,12 +268,12 @@ def tile_mix_lowrank_fm_pl_bias_kernel(tc, x, w4_words, w4_scales, down, up, b, 
         quantize(uq[1], 256, 512)
         deal_words(2, 1, 3)
         base(y1[2], 1, 2, 2)
-        for g in range(G - 1):
-            base(y1[3], 1, 3, g)
+        base(y1[3], 1, 3, 0)
         y2 = [bank(r) for r in range(3)]
         for r in range(4):
             if r == 2:
-                base(y1[3], 1, 3, G - 1)
+                base(y1[3], 1, 3, 1)
+                base(y1[3], 1, 3, 2)
                 base(y2[0], 2, 0, 0)
             branch(y1[r], 1, r)
             drain(y1[r], 1, r)
@@ -284,10 +284,10 @@ def tile_mix_lowrank_fm_pl_bias_kernel(tc, x, w4_words, w4_scales, down, up, b, 
         quantize_y(0, 0, 256)
         quantize(uq[2], 0, 128)
         quantize(uq[2], 128, 256)
-        interleave_dealt("s", u_raw[2], uq[2][0], 2, 4, 0, 88)
-        interleave_dealt("v", u_raw[2], uq[2][0], 2, 4, 88, 128)
-        interleave("s", y_f32[1], y_bf[1], 112, 128)
-        interleave("v", y_f32[0], y_bf[0], 64, 128)
+        interleave_dealt("s", u_raw[2], uq[2][0], 2, 4, 0, 80)
+        interleave_dealt("v", u_raw[2], uq[2][0], 2, 4, 80, 128)
+        interleave("s", y_f32[0], y_bf[0], 112, 128)
+        interleave("v", y_f32[0], y_bf[0], 64, 112)
         quantize(uq[2], 256, 512)
         quantize_y(0, 256, 512)
         store_words(0)
@@ -302,17 +302,15 @@ def tile_mix_lowrank_fm_pl_bias_kernel(tc, x, w4_words, w4_scales, down, up, b, 
         for g in range(1, G):
             base(y2[2], 2, 2, g)
         interleave("v", y_f32[1], y_bf[1], 0, 64)
-        interleave("v", y_f32[1], y_bf[1], 64, 112)
+        interleave("v", y_f32[1], y_bf[1], 64, 128)
         quantize_y(1, 0, 256)
         quantize_y(1, 256, 512)
         store_words(1)
         last = [bank(4 + c) for c in range(4)]
-        narrow_base(last[0], 2, 3, 0)
         branch(y2[2], 2, 2)
         drain(y2[2], 2, 2)
         for c in range(4):
-            if c:
-                narrow_base(last[c], 2, 3, 128 * c)
+            narrow_base(last[c], 2, 3, 128 * c)
             narrow_branch(last[c], 2, 3, 128 * c, "s")
         store_rows(2, 2, 4)
         interleave("v", y_f32[2], y_bf[2], 0, 32)

from contextlib import ExitStack

import concourse.mybir as mybir

K, R, M, T = 1536, 512, 1536, 512
FLOPS = 2 * T * (K * R + K * M + R * M)

F32 = mybir.dt.float32
BF16 = mybir.dt.bfloat16
I32 = mybir.dt.int32
U32 = mybir.dt.uint32
U16 = mybir.dt.uint16
U8 = mybir.dt.uint8
FP8X4 = mybir.dt.float8_e4m3fn_x4
FP4X4 = mybir.dt.float4_e2m1fn_x4
IDENT = mybir.ActivationFunctionType.Identity
ADD = mybir.AluOpType.add

P = 128
G = K // 512
A = M // 512
OUT_ROW = 4
BIAS_ROW = 8


def tile_mix_lowrank_fm_pl_bias_kernel(tc, x, w4_words, w4_scales, down, up, b, out_0, out_1, out_2):
    nc = tc.nc
    with ExitStack() as ctx:
        sb = ctx.enter_context(tc.tile_pool(name="sb", bufs=1))
        psum = ctx.enter_context(tc.psum_pool(name="psum", bufs=1))
        ctx.enter_context(tc.manual_schedule())

        def tiles(name, n, shape, dtype):
            return [sb.tile(shape, dtype, name="%s%d" % (name, i), align_bytes=256) for i in range(n)]

        w_raw = tiles("w_raw", A, [P, G, 1024], U8)
        w_dealt = tiles("w_dealt", A, [P, G, 4, 256], U8)
        s_raw = tiles("s_raw", 1, [P, G, M], U8)[0]
        s_dealt = tiles("s_dealt", 1, [P, 4, G, M // 4], U8)[0]
        b_row = tiles("b_row", 1, [P, A, 128], F32)[0]
        b_dealt = tiles("b_dealt", 1, [P, A, 128], F32)[0]
        b_turned = tiles("b_turned", 1, [P, A, 128], F32)[0]
        x_all = tiles("x_all", 1, [P, 2, 4, 512], F32)[0]
        x_raw = [x_all[:, g] for g in range(2)]
        x_last = tiles("x_last", 2, [P, 4, 256], F32)
        d_raw = tiles("d_raw", G, [P, 4, 512], F32)
        u_raw = tiles("u_raw", A, [P, 4, 512], F32)
        y_f32 = tiles("y_f32", A, [P, 4, 512], F32)

        def operand(name, n):
            return list(zip(tiles(name + "_bf", n, [P, 2048], BF16), tiles(name + "_q", n, [P, 512], U32), tiles(name + "_s", n, [P, 512], U8)))

        xq, dq, uq, hq = operand("x", G), operand("d", G), operand("u", A), operand("h", 1)[0]
        y_bf = tiles("y_bf", A, [P, 2048], BF16)
        y_q_all = tiles("y_q", 1, [P, A, 512], U32)[0]
        y_q = [y_q_all[:, a] for a in range(A)]
        y_s = tiles("y_s", 1, [P, A, 512], U8)[0]

        def bias(a, r):
            return b_turned[:, a, 32 * r + BIAS_ROW:32 * r + BIAS_ROW + 1]

        def bank(i):
            return psum.tile([P, 512], F32, name="bank%d" % i, tag="bank%d" % i)

        def copy(engine, out, in_):
            if engine == "v":
                nc.vector.tensor_copy(out=out, in_=in_)
            else:
                nc.scalar.copy(out=out, in_=in_)

        def interleave(engine, src, dst, m0, m1, run=4):
            copy(engine,
                 dst[:, 16 * m0:16 * m1].rearrange("p (m i j) -> p m j i", i=run, j=4),
                 src[:, :, 4 * m0:4 * m1].rearrange("p j (m i) -> p m j i", i=run))

        def interleave_dealt(engine, src, dst, i0, i1, m0=0, m1=128):
            copy(engine,
                 dst[:, 512 * i0:512 * i1].rearrange("p (i m j) -> p m j i", m=128, j=4)[:, m0:m1],
                 src[:].rearrange("p j (m i) -> p m j i", i=4)[:, m0:m1, :, i0:i1])

        def h_pass(g, j, c):
            cols, ts = slice(128 * j, 128 * (j + 1)), slice(128 * c, 128 * (c + 1))
            nc.tensor.matmul_mx(out=hb[c][:, cols], lhsT=dq[g][1][:, cols].bitcast(FP8X4), lhsT_scale=dq[g][2][:, cols],
                                rhs=xq[g][1][:, ts].bitcast(FP8X4), rhs_scale=xq[g][2][:, ts],
                                start=(g == 0 and j == 0), stop=(g == G - 1 and j == 3))

        def h_out(engine, c):
            copy(engine, hq[0][:, 512 * c:512 * (c + 1)].rearrange("p (t j) -> p t j", j=4), hb[c][:].rearrange("p (j t) -> p t j", j=4))

        def quantize(op, c0=0, c1=512):
            bf, q, s = op
            nc.vector.quantize_mx(out=q[:, c0:c1].bitcast(FP8X4), scales=s[:, c0:c1], in_=bf[:, 4 * c0:4 * c1])

        def mm8(acc, stat, r, mov, start, stop):
            cols = slice(128 * r, 128 * (r + 1))
            nc.tensor.matmul_mx(out=acc[:], lhsT=stat[1][:, cols].bitcast(FP8X4), lhsT_scale=stat[2][:, cols],
                                rhs=mov[1][:].bitcast(FP8X4), rhs_scale=mov[2][:], start=start, stop=stop)

        def base(acc, a, r, g):
            cols = slice(128 * a, 128 * (a + 1))
            nc.tensor.matmul_mx(out=acc[:], lhsT=w_tile(a, r, g),
                                lhsT_scale=s_dealt[:, r, g, cols],
                                rhs=xq[g][1][:].bitcast(FP8X4), rhs_scale=xq[g][2][:], start=(g == 0), stop=False)

        def branch(acc, a, r):
            mm8(acc, uq[a], r, hq, False, True)

        def deal_words(a, g0, g1):
            nc.vector.tensor_copy(out=w_dealt[a][:, g0:g1].bitcast(U16),
                                  in_=w_raw[a][:, g0:g1].bitcast(U16).rearrange("p g (m r) -> p g r m", r=4))

        def w_tile(a, r, g):
            return w_dealt[a][:, g, r].bitcast(FP4X4)

        def deal_scales(a0, a1):
            nc.vector.tensor_copy(out=s_dealt[:, :, :, 128 * a0:128 * a1],
                                  in_=s_raw[:, :, 512 * a0:512 * a1].rearrange("p g (m r) -> p r g m", r=4))

        def load_words(a):
            nc.sync.dma_start(out=w_raw[a][:].bitcast(I32),
                              in_=w4_words[:, :, 1024 * a:1024 * (a + 1)].rearrange("g p c -> p g c").bitcast(I32))

        def load_scales(r, g0, g1):
            nc.sync.dma_start(out=s_raw[r:P:32, g0:g1].bitcast(I32),
                              in_=w4_scales[g0:g1, r:16:4].rearrange("g q n -> q g n").bitcast(I32))

        def load_rows(dst, rows):
            nc.sync.dma_start(out=dst[:], in_=rows.rearrange("(p j) c -> p j c", j=4))

        def narrow_base(acc, a, r, c0):
            cols, ts = slice(128 * a, 128 * (a + 1)), slice(c0, c0 + 128)
            for g in range(G):
                nc.tensor.matmul_mx(out=acc[:, 0:128], lhsT=w_tile(a, r, g),
                                    lhsT_scale=s_dealt[:, r, g, cols],
                                    rhs=xq[g][1][:, ts].bitcast(FP8X4), rhs_scale=xq[g][2][:, ts], start=(g == 0), stop=False)

        def narrow_branch(acc, a, r, c0, engine):
            cols, ts = slice(128 * r, 128 * (r + 1)), slice(c0, c0 + 128)
            nc.tensor.matmul_mx(out=acc[:, 0:128], lhsT=uq[a][1][:, cols].bitcast(FP8X4), lhsT_scale=uq[a][2][:, cols],
                                rhs=hq[1][:, ts].bitcast(FP8X4), rhs_scale=hq[2][:, ts], start=False, stop=True)
            if engine == "v":
                nc.vector.tensor_scalar(out=y_f32[a][:, r, ts], in0=acc[:, 0:128], scalar1=bias(a, r), scalar2=None, op0=ADD)
            else:
                nc.scalar.activation(out=y_f32[a][:, r, ts], in_=acc[:, 0:128], func=IDENT, bias=bias(a, r))

        def drain_v(acc, a, r):
            nc.vector.tensor_scalar(out=y_f32[a][:, r, :], in0=acc[:], scalar1=bias(a, r), scalar2=None, op0=ADD)

        def drain(acc, a, r):
            nc.scalar.activation(out=y_f32[a][:, r, :], in_=acc[:], func=IDENT, bias=bias(a, r))

        def store_rows(a, r0, r1):
            rows = out_0[512 * a:512 * (a + 1), :].rearrange("(p r) t -> p r t", r=4)
            nc.sync.dma_start(out=rows[:, r0:r1, :], in_=y_f32[a][:, r0:r1, :])

        def quantize_y(a, c0=0, c1=512):
            nc.vector.quantize_mx(out=y_q[a][:, c0:c1].bitcast(FP8X4), scales=y_s[OUT_ROW:P, a, c0:c1], in_=y_bf[a][:, 4 * c0:4 * c1])

        def store_words(a, c0=0, c1=512):
            nc.sync.dma_start(out=out_1[a, :, c0:c1, :].rearrange("p t i -> p (t i)").bitcast(I32), in_=y_q[a][:, c0:c1].bitcast(I32))

        def store_words_of(a0, a1):
            nc.sync.dma_start(out=out_1[a0:a1].rearrange("a p t i -> p a (t i)").bitcast(I32), in_=y_q_all[:, a0:a1].bitcast(I32))

        def store_scales(queue, a0, a1, r):
            queue.dma_start(out=out_2[a0:a1, r:16:4, :].rearrange("a q t -> q a t").bitcast(I32),
                            in_=y_s[OUT_ROW + r:P:32, a0:a1, :].bitcast(I32))

        def round_last(engine, h, m0, m1):
            interleave(engine, x_last[h], xq[2][0][:, 1024 * h:1024 * (h + 1)], m0, m1)

        def half_base(acc, r, h):
            ts = slice(256 * h, 256 * (h + 1))
            nc.tensor.matmul_mx(out=acc[:, ts], lhsT=w_tile(0, r, 2), lhsT_scale=s_dealt[:, r, 2, 0:128],
                                rhs=xq[2][1][:, ts].bitcast(FP8X4), rhs_scale=xq[2][2][:, ts], start=False, stop=False)

        nc.vector.memset(s_raw[:].rearrange("p g n -> p (g n)").bitcast(I32), 0)
        nc.vector.memset(b_row[:].rearrange("p a c -> p (a c)"), 0.0)
        load_words(0)
        for r in range(4):
            load_scales(r, 0, 3)
        nc.sync.dma_start(out=b_row[BIAS_ROW:P:32], in_=b.rearrange("(a q c) -> q a c", a=A, q=4))
        nc.sync.dma_start(out=x_all[:], in_=x[0:1024, :].rearrange("(g p j) c -> p g j c", g=2, j=4))
        for g in range(G):
            load_rows(d_raw[g], down[512 * g:512 * (g + 1), :])
        for h in range(2):
            load_rows(x_last[h], x[1024:1536, 256 * h:256 * (h + 1)])
        load_words(1)
        load_rows(u_raw[0], up[:, 0:512])
        load_rows(u_raw[1], up[:, 512:1024])
        load_words(2)
        load_rows(u_raw[2], up[:, 1024:1536])

        y0 = [bank(r) for r in range(4)]
        hb = [bank(4 + c) for c in range(4)]

        deal_words(0, 0, 2)
        deal_words(0, 2, 3)
        deal_scales(0, 3)
        nc.vector.tensor_copy(out=b_dealt[:].rearrange("p a (r m) -> p a r m", r=4), in_=b_row[:].rearrange("p a (m r) -> p a r m", r=4))
        for a in range(A):
            nc.vector.transpose(out=b_turned[:, a], in_=b_dealt[:, a])
        interleave("s", x_raw[0], xq[0][0], 88, 128)
        interleave("v", x_raw[0], xq[0][0], 0, 88)
        interleave("s", x_raw[1], xq[1][0], 40, 128)
        interleave("v", x_raw[1], xq[1][0], 0, 40)
        quantize(xq[0])
        for r in range(4):
            base(y0[r], 0, r, 0)
        for g in range(G):
            interleave_dealt("s", d_raw[g], dq[g][0], 0, 2, 88, 128)
            interleave_dealt("v", d_raw[g], dq[g][0], 0, 2, 0, 88)
            interleave_dealt("s", d_raw[g], dq[g][0], 2, 4, 0, 56)
            interleave_dealt("v", d_raw[g], dq[g][0], 2, 4, 56, 128)
            quantize(dq[g], 0, 256)
            quantize(dq[g], 256, 512)
            if g == 0:
                quantize(xq[1])
            if g < 2:
                for c in range(4):
                    for j in range(4):
                        h_pass(g, j, c)
        for r in range(4):
            base(y0[r], 0, r, 1)
        for h in range(2):
            round_last("s", h, 40, 64)
            round_last("v", h, 0, 40)
            quantize(xq[2], 256 * h, 256 * h + 128)
            quantize(xq[2], 256 * h + 128, 256 * h + 256)
            for c in range(2 * h, 2 * h + 2):
                for j in range(4):
                    h_pass(2, j, c)
            for r in range(4):
                half_base(y0[r], r, h)
        h_out("s", 0)
        h_out("s", 1)
        deal_words(1, 0, 2)
        deal_words(1, 2, 3)
        h_out("s", 2)
        quantize(hq, 0, 256)
        h_out("v", 3)
        y1 = [bank(4 + r) for r in range(4)]
        interleave_dealt("s", u_raw[0], uq[0][0], 0, 2, 88, 128)
        interleave_dealt("v", u_raw[0], uq[0][0], 0, 2, 0, 88)
        quantize(hq, 256, 512)
        quantize(uq[0], 0, 128)
        quantize(uq[0], 128, 256)
        interleave_dealt("s", u_raw[0], uq[0][0], 2, 4, 0, 96)
        interleave_dealt("v", u_raw[0], uq[0][0], 2, 4, 96, 128)
        quantize(uq[0], 256, 512)
        for r in range(2):
            for g in range(G):
                base(y1[r], 1, r, g)
        for r in range(4):
            if r == 2:
                base(y1[2], 1, 2, 0)
                base(y1[2], 1, 2, 1)
            branch(y0[r], 0, r)
            drain(y0[r], 0, r)
            if r % 2:
                store_rows(0, r - 1, r + 1)
        interleave_dealt("v", u_raw[1], uq[1][0], 0, 2)
        interleave_dealt("v", u_raw[1], uq[1][0], 2, 4, 0, 64)
        quantize(uq[1], 0, 128)
        quantize(uq[1], 128, 256)
        interleave_dealt("v", u_raw[1], uq[1][0], 2, 4, 64, 128)
        deal_words(2, 0, 1)
        quantize(uq[1], 256, 512)
        deal_words(2, 1, 3)
        base(y1[2], 1, 2, 2)
        base(y1[3], 1, 3, 0)
        y2 = [bank(r) for r in range(3)]
        for r in range(4):
            if r == 2:
                base(y1[3], 1, 3, 1)
                base(y1[3], 1, 3, 2)
                base(y2[0], 2, 0, 0)
            branch(y1[r], 1, r)
            drain(y1[r], 1, r)
            if r % 2:
                store_rows(1, r - 1, r + 1)
        interleave("v", y_f32[0], y_bf[0], 0, 64)
        interleave_dealt("v", u_raw[2], uq[2][0], 0, 2)
        quantize_y(0, 0, 256)
        quantize(uq[2], 0, 128)
        quantize(uq[2], 128, 256)
        interleave_dealt("s", u_raw[2], uq[2][0], 2, 4, 0, 80)
        interleave_dealt("v", u_raw[2], uq[2][0], 2, 4, 80, 128)
        interleave("s", y_f32[0], y_bf[0], 112, 128)
        interleave("v", y_f32[0], y_bf[0], 64, 112)
        quantize(uq[2], 256, 512)
        quantize_y(0, 256, 512)
        store_words(0)
        for r in range(2):
            for g in range(1 - r, G):
                base(y2[r], 2, r, g)
        base(y2[2], 2, 2, 0)
        for r in range(2):
            branch(y2[r], 2, r)
            drain(y2[r], 2, r)
        store_rows(2, 0, 2)
        for g in range(1, G):
            base(y2[2], 2, 2, g)
        interleave("v", y_f32[1], y_bf[1], 0, 64)
        interleave("v", y_f32[1], y_bf[1], 64, 128)
        quantize_y(1, 0, 256)
        quantize_y(1, 256, 512)
        store_words(1)
        last = [bank(4 + c) for c in range(4)]
        branch(y2[2], 2, 2)
        drain(y2[2], 2, 2)
        for c in range(4):
            narrow_base(last[c], 2, 3, 128 * c)
            narrow_branch(last[c], 2, 3, 128 * c, "s")
        store_rows(2, 2, 4)
        interleave("v", y_f32[2], y_bf[2], 0, 32)
        interleave("v", y_f32[2], y_bf[2], 32, 64)
        interleave("s", y_f32[2], y_bf[2], 64, 96)
        interleave("v", y_f32[2], y_bf[2], 96, 128)
        quantize_y(2, 0, 256)
        quantize_y(2, 256, 512)
        for q in range(4):
            store_scales(nc.scalar if q % 2 else nc.sync, 0, 3, q)
        store_words(2)
